import numpy as np
import ml_dtypes


def mxq(x, axis, fmt="e4m3"):
    dtype, down = {"e4m3": (ml_dtypes.float8_e4m3fn, 7), "e5m2": (ml_dtypes.float8_e5m2, 14)}[fmt]
    v = np.moveaxis(np.asarray(x, np.float32).astype(ml_dtypes.bfloat16).astype(np.float64), axis, -1)
    blocks = v.reshape(v.shape[:-1] + (-1, 32))
    amax = np.abs(blocks).max(-1, keepdims=True)
    byte = np.maximum(np.where(amax > 0, np.frexp(amax)[1] - 1 + 127, 0) - down, 1)
    scale = np.exp2(byte - 127.0)
    codes = (blocks / scale).astype(np.float32).astype(dtype).astype(np.float64)
    return np.moveaxis((codes * scale).reshape(v.shape), -1, axis)


WIDE = False


def mx_kscale(k):
    if not WIDE:
        return np.ones(k)
    levels = np.array([10, -10, 5, -5, 0])
    if k % 512:
        return np.exp2(np.random.permutation(np.resize(levels, k // 32))).repeat(32)
    a = np.empty((k // 512, 16))
    for p in range(k // 512):
        a[p, :8] = np.random.permutation(np.resize(levels, 8))
        for g in range(8):
            far = levels[np.abs(levels - a[p, g]) >= 10]
            a[p, g + 8] = far[np.random.randint(len(far))]
    return np.exp2(a.ravel()).repeat(32)


def f64(x):
    return np.asarray(x).astype(np.float64)


def striped(idx):
    return np.tile(idx.reshape(-1, 16).T, (8, 1)).astype(np.uint16)


def unstriped(offs):
    return offs[:16].T.reshape(-1).astype(np.int64)


E2M1 = np.array([0.0, 0.5, 1.0, 1.5, 2.0, 3.0, 4.0, 6.0, -0.0, -0.5, -1.0, -1.5, -2.0, -3.0, -4.0, -6.0])


def pack_weight(w, fmt):
    k, n = w.shape
    w = f64(np.asarray(w, np.float32).astype(ml_dtypes.bfloat16)).reshape(k // 32, 32, n)
    amax = np.abs(w).max(1)
    if fmt == "e4m3":
        byte = np.frexp(amax)[1] - 1 + 127 - 7
    else:
        mant, ex = np.frexp(amax / 6.0)
        byte = np.where(mant > 0.5, ex, ex - 1) + 127
    byte = np.clip(np.where(amax > 0, byte, 1), 1, 254)
    scaled = (w * np.exp2(127.0 - byte)[:, None, :]).reshape(k, n).astype(np.float32)
    by_word = np.ascontiguousarray(scaled.reshape(k // 512, 128, 4, n).transpose(0, 1, 3, 2))
    if fmt == "e4m3":
        words = by_word.astype(ml_dtypes.float8_e4m3fn).view(np.uint8)
    else:
        c = by_word.astype(ml_dtypes.float4_e2m1fn).view(np.uint8) & 0xF
        words = (c[..., 0::2] | (c[..., 1::2] << 4)).reshape(k // 512, 128, 2 * n)
    return np.ascontiguousarray(words), np.ascontiguousarray(byte.astype(np.uint8).reshape(k // 512, 16, n))


def unpack_weight(words, scales, fmt):
    g, _, n = scales.shape
    words = np.ascontiguousarray(words).reshape(g, 128, n, -1)
    if fmt == "e4m3":
        vals = words.view(ml_dtypes.float8_e4m3fn).astype(np.float64)
    else:
        nib = np.empty((g, 128, n, 4), np.uint8)
        nib[..., 0::2] = words & 0xF
        nib[..., 1::2] = words >> 4
        vals = E2M1[nib]
    vals = vals * np.repeat(np.exp2(scales.astype(np.float64) - 127.0), 8, axis=1)[..., None]
    return vals.transpose(0, 1, 3, 2).reshape(g * 512, n)


def gelu(v):
    return 0.5 * v * (1.0 + np.tanh(np.sqrt(2.0 / np.pi) * (v + 0.044715 * v**3)))


K, H, N, T, S, T2 = 1024, 1024, 384, 2048, 1024, 2048

def setup_inputs():
    n = np.random.standard_normal
    s = mx_kscale(K)[:, None]
    u = mx_kscale(H)[:, None]
    tab_words, tab_scales = pack_weight(n((K, T)) * s, "e4m3")
    w_even = (n((K, H)) / np.sqrt(K) / s * u.T).astype(np.float32)
    w_odd_words, w_odd_scales = pack_weight(n((K, H)) / np.sqrt(K) / s * u.T, "e2m1")
    w_pool_words, w_pool_scales = pack_weight(n((H, N)) / np.sqrt(H) / u, "e4m3")
    wgo = np.exp(0.3 * n((128, S))).astype(np.float32)
    return {"tab_words": tab_words, "tab_scales": tab_scales,
            "offs": striped(np.random.permutation(T)[:S]),
            "w_even": w_even,
            "w_odd_words": w_odd_words, "w_odd_scales": w_odd_scales,
            "w_pool_words": w_pool_words, "w_pool_scales": w_pool_scales,
            "wgo": wgo,
            "offs2": striped(np.random.permutation(T2)[:S])}

def reference(tab_words, tab_scales, offs, w_even, w_odd_words, w_odd_scales,
              w_pool_words, w_pool_scales, wgo, offs2):
    v = unpack_weight(tab_words, tab_scales, "e4m3")[:, unstriped(offs)]
    we = mxq(f64(w_even), 0, "e4m3")
    wo = unpack_weight(w_odd_words, w_odd_scales, "e2m1")
    wp = unpack_weight(w_pool_words, w_pool_scales, "e4m3")
    e = we.T @ v
    o = wo.T @ v
    h = np.sqrt(e * e + o * o)
    y = wp.T @ mxq(h, 0, "e4m3")
    out = np.zeros((N, T2))
    out[:, unstriped(offs2)] = np.tile(f64(wgo), (N // 128, 1)) * y
    return out

@@ -1,0 +1,207 @@
+from contextlib import ExitStack
+
+import concourse.mybir as mybir
+from concourse.masks import make_identity
+
+K, H, N, T, S, T2 = 1024, 1024, 384, 2048, 1024, 2048
+FLOPS = 2 * 2 * K * H * S + 2 * H * N * S
+
+F32 = mybir.dt.float32
+BF16 = mybir.dt.bfloat16
+I32 = mybir.dt.int32
+U32 = mybir.dt.uint32
+U16 = mybir.dt.uint16
+U8 = mybir.dt.uint8
+FP8X4 = mybir.dt.float8_e4m3fn_x4
+FP4X4 = mybir.dt.float4_e2m1fn_x4
+ACT = mybir.ActivationFunctionType
+MULT = mybir.AluOpType.mult
+ADD = mybir.AluOpType.add
+
+P = 128
+PACK = 4
+PASS = P * PACK
+K_PASSES = K // PASS
+H_PASSES = H // PASS
+CHUNK = 256
+CHUNKS = S // CHUNK
+TILES = CHUNK // P
+PAGES = N // P
+LIST_COLS = CHUNK // 16
+
+
+def tile_list_orientation_energy_store_kernel(
+    tc, tab_words, tab_scales, offs, w_even, w_odd_words, w_odd_scales, w_pool_words, w_pool_scales, wgo, offs2, out
+):
+    nc = tc.nc
+    with ExitStack() as ctx:
+        keep = ctx.enter_context(tc.tile_pool(name="keep", bufs=1))
+        ring = ctx.enter_context(tc.tile_pool(name="ring", bufs=4))
+        psum = ctx.enter_context(tc.psum_pool(name="psum", bufs=2))
+
+        pick_list = keep.tile([P, S // 16], U16, name="pick_list")
+        nc.sync.dma_start(pick_list[:], offs)
+        place_list = keep.tile([P, S // 16], U16, name="place_list")
+        nc.sync.dma_start(place_list[:], offs2)
+
+        ident = keep.tile([P, P], F32, name="ident")
+        tab_sc = keep.tile([P, K_PASSES, T], U8, name="tab_sc", align_bytes=64)
+        odd_sc = keep.tile([P, K_PASSES, H], U8, name="odd_sc", align_bytes=64)
+        nc.vector.memset(tab_sc[:].bitcast(I32), 0)
+        nc.gpsimd.memset(odd_sc[:].bitcast(I32), 0)
+        make_identity(nc, ident[:])
+
+        def load_scale_rows(plane, scales):
+            for q in range(4):
+                nc.sync.dma_start(
+                    out=plane[32 * q : 32 * q + 4, :, :].bitcast(I32),
+                    in_=scales[:, 4 * q : 4 * q + 4, :].rearrange("a r c -> r a c").bitcast(I32),
+                )
+
+        tab_w = [keep.tile([P, T], I32, name=f"tab_w{a}", align_bytes=64) for a in range(K_PASSES)]
+        odd_w = [keep.tile([P, 2 * H], U8, name=f"odd_w{a}", align_bytes=64) for a in range(K_PASSES)]
+        for a in range(K_PASSES):
+            words = tab_words[a].rearrange("p t i -> p (t i)").bitcast(I32)
+            for cols in (slice(0, T // 2), slice(T // 2, T)):
+                nc.sync.dma_start(out=tab_w[a][:, cols], in_=words[:, cols])
+        for a in range(K_PASSES):
+            nc.sync.dma_start(out=odd_w[a][:].bitcast(I32), in_=w_odd_words[a].bitcast(I32))
+        load_scale_rows(tab_sc, tab_scales)
+        load_scale_rows(odd_sc, w_odd_scales)
+
+        warm_in = keep.tile([P, 1], F32, name="warm_in")
+        warm_out = keep.tile([P, 1], F32, name="warm_out")
+        nc.vector.memset(warm_in[:], 1.0)
+        nc.scalar.activation(out=warm_out[:], in_=warm_in[:], func=ACT.Sqrt)
+
+        def gather_patches(c):
+            picks = pick_list[:, c * LIST_COLS : (c + 1) * LIST_COLS]
+            patch_w, patch_sc = [], []
+            for a in range(K_PASSES):
+                words = ring.tile([P, CHUNK], U32, name=f"patch_w{a}", align_bytes=64, bufs=3)
+                nc.vector.tensor_copy(out=words[:], in_=tab_w[a][:].bitcast(U32).indirect(picks))
+                plane = ring.tile([P, CHUNK], U8, name=f"patch_sc{a}", align_bytes=64, bufs=3)
+                nc.vector.tensor_copy(out=plane[:], in_=tab_sc[:, a, :].indirect(picks))
+                patch_w.append(words)
+                patch_sc.append(plane)
+            return patch_w, patch_sc
+
+        patches = [gather_patches(c) for c in range(3)]
+
+        even_w, even_sc = {}, {}
+        for b in range(H_PASSES):
+            for a in range(K_PASSES):
+                raw = keep.tile([P, PACK, PASS], F32, name=f"even_raw{b}_{a}")
+                rows = w_even[a * PASS : (a + 1) * PASS, b * PASS : (b + 1) * PASS]
+                nc.sync.dma_start(out=raw[:], in_=rows.rearrange("(p i) r -> p i r", i=PACK))
+                rounded = keep.tile([P, PASS * PACK], BF16, name=f"even_bf{b}_{a}", align_bytes=64)
+                nc.vector.tensor_copy(
+                    out=rounded[:].rearrange("p (g u i) -> p g i u", u=4, i=PACK),
+                    in_=raw[:].rearrange("p i (g u) -> p g i u", u=4),
+                )
+                codes = keep.tile([P, PASS], U32, name=f"even_w{b}_{a}", align_bytes=64)
+                scales = keep.tile([P, PASS], U8, name=f"even_sc{b}_{a}", align_bytes=64)
+                nc.vector.quantize_mx(out=codes[:].bitcast(FP8X4), scales=scales[:], in_=rounded[:])
+                even_w[b, a], even_sc[b, a] = codes, scales
+
+        pool_w = keep.tile([P, H_PASSES, N], I32, name="pool_w", align_bytes=64)
+        nc.sync.dma_start(out=pool_w[:], in_=w_pool_words.rearrange("b p c i -> p b (c i)").bitcast(I32))
+        pool_sc = keep.tile([P, N], U8, name="pool_sc", align_bytes=64)
+        nc.gpsimd.memset(pool_sc[:].bitcast(I32), 0)
+        for q in range(4):
+            nc.gpsimd.dma_start(
+                out=pool_sc[32 * q : 32 * q + 8, :].bitcast(I32), in_=w_pool_scales[:, 4 * q : 4 * q + 4, :].bitcast(I32)
+            )
+        gain = keep.tile([P, S], F32, name="gain")
+        nc.sync.dma_start(out=gain[:], in_=wgo)
+
+        pages = []
+        for n in range(PAGES):
+            page = keep.tile([P, T2], F32, name=f"page{n}")
+            nc.gpsimd.memset(page[:], 0.0)
+            pages.append(page)
+
+        def squared_response(patch_w, patch_sc, jt, tag, moving, moving_sc, squares):
+            cols = slice(jt * P, (jt + 1) * P)
+            bank = psum.tile([P, PASS], F32, name=tag)
+            for a in range(K_PASSES):
+                nc.tensor.matmul_mx(
+                    out=bank[:],
+                    lhsT=patch_w[a][:, cols].bitcast(FP8X4),
+                    lhsT_scale=patch_sc[a][:, cols],
+                    rhs=moving[a],
+                    rhs_scale=moving_sc[a],
+                    start=(a == 0),
+                    stop=(a == K_PASSES - 1),
+                )
+            nc.scalar.activation(
+                out=squares[:], in_=bank[:].rearrange("p (m t) -> p t m", t=PACK), func=ACT.Square
+            )
+
+        for c in range(CHUNKS):
+            if c + 3 - 1 < CHUNKS and c > 0:
+                patches.append(gather_patches(c + 3 - 1))
+            patch_w, patch_sc = patches[c]
+            amp_w, amp_sc = [], []
+            for b in range(H_PASSES):
+                amp = keep.tile([P, CHUNK * PACK], BF16, name=f"amp{c}_{b}", align_bytes=64)
+                for jt in range(TILES):
+                    odd_sq = keep.tile([P, PACK, P], F32, name=f"odd_sq{c}_{b}_{jt}")
+                    squared_response(
+                        patch_w, patch_sc, jt, "odd_bank",
+                        [odd_w[a][:, 2 * b * PASS : 2 * (b + 1) * PASS].bitcast(FP4X4) for a in range(K_PASSES)],
+                        [odd_sc[:, a, b * PASS : (b + 1) * PASS] for a in range(K_PASSES)],
+                        odd_sq,
+                    )
+                    even_sq = ring.tile([P, PACK, P], F32, name="even_sq")
+                    squared_response(
+                        patch_w, patch_sc, jt, "even_bank",
+                        [even_w[b, a][:].bitcast(FP8X4) for a in range(K_PASSES)],
+                        [even_sc[b, a][:] for a in range(K_PASSES)],
+                        even_sq,
+                    )
+                    energy = psum.tile([P, PACK, P], F32, name="energy")
+                    if b == 0:
+                        both = ring.tile([P, PACK, P], F32, name="both")
+                        nc.vector.tensor_tensor(both[:], odd_sq[:], even_sq[:], ADD)
+                        for t in range(PACK):
+                            nc.tensor.transpose(energy[:, t, :], both[:, t, :], ident[:])
+                    else:
+                        for t in range(PACK):
+                            nc.tensor.matmul(energy[:, t, :], lhsT=odd_sq[:, t, :], rhs=ident[:], is_transpose=True, start=True, stop=False)
+                            nc.tensor.matmul(energy[:, t, :], lhsT=even_sq[:, t, :], rhs=ident[:], is_transpose=True, start=False, stop=True)
+                    nc.scalar.activation(
+                        out=amp[:, jt * PASS : (jt + 1) * PASS].rearrange("p (j t) -> p j t", t=PACK),
+                        in_=energy[:].rearrange("p t j -> p j t"),
+                        func=ACT.Sqrt,
+                    )
+                codes = keep.tile([P, CHUNK], U32, name=f"amp_w{c}_{b}", align_bytes=64)
+                scales = keep.tile([P, CHUNK], U8, name=f"amp_sc{c}_{b}", align_bytes=64)
+                nc.vector.quantize_mx(out=codes[:].bitcast(FP8X4), scales=scales[:], in_=amp[:])
+                amp_w.append(codes)
+                amp_sc.append(scales)
+
+            for n in range(PAGES):
+                cols = slice(n * P, (n + 1) * P)
+                pooled = psum.tile([P, CHUNK], F32, name="pooled")
+                for b in range(H_PASSES):
+                    nc.tensor.matmul_mx(
+                        out=pooled[:],
+                        lhsT=pool_w[:, b, cols].bitcast(FP8X4),
+                        lhsT_scale=pool_sc[4 * b : P, cols],
+                        rhs=amp_w[b][:].bitcast(FP8X4),
+                        rhs_scale=amp_sc[b][:],
+                        start=(b == 0),
+                        stop=(b == H_PASSES - 1),
+                    )
+                y = keep.tile([P, CHUNK], F32, name=f"y{c}_{n}")
+                nc.scalar.copy(out=y[:], in_=pooled[:])
+                nc.vector.tensor_tensor(
+                    pages[n][:].indirect(place_list[:, c * LIST_COLS : (c + 1) * LIST_COLS]),
+                    y[:],
+                    gain[:, c * CHUNK : (c + 1) * CHUNK],
+                    MULT,
+                )
+
+        for n in range(PAGES):
+            nc.sync.dma_start(out=out[n * P : (n + 1) * P, :], in_=pages[n][:])

@@ -28,6 +28,7 @@ CHUNKS = S // CHUNK
 TILES = CHUNK // P
 PAGES = N // P
 LIST_COLS = CHUNK // 16
+BANKS = 8
 
 
 def tile_list_orientation_energy_store_kernel(
@@ -36,172 +37,202 @@ def tile_list_orientation_energy_store_kernel(
     nc = tc.nc
     with ExitStack() as ctx:
         keep = ctx.enter_context(tc.tile_pool(name="keep", bufs=1))
-        ring = ctx.enter_context(tc.tile_pool(name="ring", bufs=4))
-        psum = ctx.enter_context(tc.psum_pool(name="psum", bufs=2))
+        psum = ctx.enter_context(tc.psum_pool(name="psum", bufs=1))
 
         pick_list = keep.tile([P, S // 16], U16, name="pick_list")
         nc.sync.dma_start(pick_list[:], offs)
         place_list = keep.tile([P, S // 16], U16, name="place_list")
         nc.sync.dma_start(place_list[:], offs2)
 
-        ident = keep.tile([P, P], F32, name="ident")
-        tab_sc = keep.tile([P, K_PASSES, T], U8, name="tab_sc", align_bytes=64)
-        odd_sc = keep.tile([P, K_PASSES, H], U8, name="odd_sc", align_bytes=64)
+        tab_sc = keep.tile([P, T], U8, name="tab_sc", tag="scales_then_floats", align_bytes=64)
         nc.vector.memset(tab_sc[:].bitcast(I32), 0)
+        for q in range(4):
+            nc.scalar.dma_start(
+                out=tab_sc[32 * q : 32 * q + 8, :].bitcast(I32), in_=tab_scales[:, 4 * q : 4 * q + 4, :].bitcast(I32)
+            )
+        tab_w = keep.tile([P, K_PASSES, T], I32, name="tab_w", tag="words", align_bytes=64)
+        nc.sync.dma_start(out=tab_w[:], in_=tab_words.rearrange("a p t i -> p a (t i)").bitcast(I32))
+        odd_w = keep.tile([P, K_PASSES, 2 * H], U8, name="odd_w", align_bytes=64)
+        nc.sync.dma_start(out=odd_w[:].bitcast(I32), in_=w_odd_words.rearrange("a p c -> p a c").bitcast(I32))
+
+        odd_sc = keep.tile([P, K_PASSES, H], U8, name="odd_sc", align_bytes=64)
         nc.gpsimd.memset(odd_sc[:].bitcast(I32), 0)
+        for q in range(4):
+            nc.gpsimd.dma_start(
+                out=odd_sc[32 * q : 32 * q + 4, :, :].bitcast(I32),
+                in_=w_odd_scales[:, 4 * q : 4 * q + 4, :].rearrange("a r c -> r a c").bitcast(I32),
+            )
+        ident = keep.tile([P, P], F32, name="ident")
         make_identity(nc, ident[:])
-
-        def load_scale_rows(plane, scales):
-            for q in range(4):
-                nc.sync.dma_start(
-                    out=plane[32 * q : 32 * q + 4, :, :].bitcast(I32),
-                    in_=scales[:, 4 * q : 4 * q + 4, :].rearrange("a r c -> r a c").bitcast(I32),
-                )
-
-        tab_w = [keep.tile([P, T], I32, name=f"tab_w{a}", align_bytes=64) for a in range(K_PASSES)]
-        odd_w = [keep.tile([P, 2 * H], U8, name=f"odd_w{a}", align_bytes=64) for a in range(K_PASSES)]
-        for a in range(K_PASSES):
-            words = tab_words[a].rearrange("p t i -> p (t i)").bitcast(I32)
-            for cols in (slice(0, T // 2), slice(T // 2, T)):
-                nc.sync.dma_start(out=tab_w[a][:, cols], in_=words[:, cols])
-        for a in range(K_PASSES):
-            nc.sync.dma_start(out=odd_w[a][:].bitcast(I32), in_=w_odd_words[a].bitcast(I32))
-        load_scale_rows(tab_sc, tab_scales)
-        load_scale_rows(odd_sc, w_odd_scales)
-
-        warm_in = keep.tile([P, 1], F32, name="warm_in")
-        warm_out = keep.tile([P, 1], F32, name="warm_out")
-        nc.vector.memset(warm_in[:], 1.0)
-        nc.scalar.activation(out=warm_out[:], in_=warm_in[:], func=ACT.Sqrt)
-
-        def gather_patches(c):
-            picks = pick_list[:, c * LIST_COLS : (c + 1) * LIST_COLS]
-            patch_w, patch_sc = [], []
-            for a in range(K_PASSES):
-                words = ring.tile([P, CHUNK], U32, name=f"patch_w{a}", align_bytes=64, bufs=3)
-                nc.vector.tensor_copy(out=words[:], in_=tab_w[a][:].bitcast(U32).indirect(picks))
-                plane = ring.tile([P, CHUNK], U8, name=f"patch_sc{a}", align_bytes=64, bufs=3)
-                nc.vector.tensor_copy(out=plane[:], in_=tab_sc[:, a, :].indirect(picks))
-                patch_w.append(words)
-                patch_sc.append(plane)
-            return patch_w, patch_sc
-
-        patches = [gather_patches(c) for c in range(3)]
-
-        even_w, even_sc = {}, {}
-        for b in range(H_PASSES):
-            for a in range(K_PASSES):
-                raw = keep.tile([P, PACK, PASS], F32, name=f"even_raw{b}_{a}")
-                rows = w_even[a * PASS : (a + 1) * PASS, b * PASS : (b + 1) * PASS]
-                nc.sync.dma_start(out=raw[:], in_=rows.rearrange("(p i) r -> p i r", i=PACK))
-                rounded = keep.tile([P, PASS * PACK], BF16, name=f"even_bf{b}_{a}", align_bytes=64)
-                nc.vector.tensor_copy(
-                    out=rounded[:].rearrange("p (g u i) -> p g i u", u=4, i=PACK),
-                    in_=raw[:].rearrange("p i (g u) -> p g i u", u=4),
-                )
-                codes = keep.tile([P, PASS], U32, name=f"even_w{b}_{a}", align_bytes=64)
-                scales = keep.tile([P, PASS], U8, name=f"even_sc{b}_{a}", align_bytes=64)
-                nc.vector.quantize_mx(out=codes[:].bitcast(FP8X4), scales=scales[:], in_=rounded[:])
-                even_w[b, a], even_sc[b, a] = codes, scales
-
-        pool_w = keep.tile([P, H_PASSES, N], I32, name="pool_w", align_bytes=64)
-        nc.sync.dma_start(out=pool_w[:], in_=w_pool_words.rearrange("b p c i -> p b (c i)").bitcast(I32))
+        pages = []
+        for n in range(PAGES):
+            page = keep.tile([P, T2], F32, name=f"page{n}")
+            nc.gpsimd.memset(page[:], 0.0)
+            pages.append(page)
         pool_sc = keep.tile([P, N], U8, name="pool_sc", align_bytes=64)
         nc.gpsimd.memset(pool_sc[:].bitcast(I32), 0)
         for q in range(4):
             nc.gpsimd.dma_start(
                 out=pool_sc[32 * q : 32 * q + 8, :].bitcast(I32), in_=w_pool_scales[:, 4 * q : 4 * q + 4, :].bitcast(I32)
             )
-        gain = keep.tile([P, S], F32, name="gain")
-        nc.sync.dma_start(out=gain[:], in_=wgo)
 
-        pages = []
-        for n in range(PAGES):
-            page = keep.tile([P, T2], F32, name=f"page{n}")
-            nc.gpsimd.memset(page[:], 0.0)
-            pages.append(page)
+        warm_in = keep.tile([P, 1], F32, name="warm_in")
+        warm_out = keep.tile([P, 1], F32, name="warm_out")
+        nc.vector.memset(warm_in[:], 1.0)
+        nc.scalar.activation(out=warm_out[:], in_=warm_in[:], func=ACT.Sqrt)
 
-        def squared_response(patch_w, patch_sc, jt, tag, moving, moving_sc, squares):
-            cols = slice(jt * P, (jt + 1) * P)
-            bank = psum.tile([P, PASS], F32, name=tag)
+        picked_sc, second_sc = [], []
+        for half in range(2):
+            shifted = keep.tile([P, S // 2], U8, name=f"second_sc{half}", align_bytes=64)
+            nc.vector.memset(shifted[:].bitcast(I32), 0)
+            picked = keep.tile([P, S // 2], U8, name=f"picked_sc{half}", align_bytes=64)
+            nc.vector.tensor_copy(out=picked[:], in_=tab_sc[:].indirect(pick_list[:, half * 32 : (half + 1) * 32]))
+            nc.scalar.dma_start(out=shifted[0 : P - 4, :].bitcast(I32), in_=picked[4:P, :].bitcast(I32))
+            picked_sc.append(picked)
+            second_sc.append(shifted)
+
+        patch_w = {}
+        for c in range(CHUNKS):
             for a in range(K_PASSES):
-                nc.tensor.matmul_mx(
-                    out=bank[:],
-                    lhsT=patch_w[a][:, cols].bitcast(FP8X4),
-                    lhsT_scale=patch_sc[a][:, cols],
-                    rhs=moving[a],
-                    rhs_scale=moving_sc[a],
-                    start=(a == 0),
-                    stop=(a == K_PASSES - 1),
+                picked = keep.tile([P, CHUNK], U32, name=f"patch_w{c}_{a}", align_bytes=64)
+                nc.vector.tensor_copy(
+                    out=picked[:],
+                    in_=tab_w[:, a, :].bitcast(U32).indirect(pick_list[:, c * LIST_COLS : (c + 1) * LIST_COLS]),
                 )
-            nc.scalar.activation(
-                out=squares[:], in_=bank[:].rearrange("p (m t) -> p t m", t=PACK), func=ACT.Square
+                patch_w[c, a] = picked
+
+        piece = PACK * PASS
+        floats = keep.tile(
+            [P, H_PASSES * K_PASSES * piece + S], F32, name="floats", tag="scales_then_floats", align_bytes=64
+        )
+        even_w, even_sc = {}, {}
+        for b in range(H_PASSES):
+            for a in range(K_PASSES):
+                first = (b * K_PASSES + a) * piece
+                raw = floats[:, first : first + piece]
+                rows = w_even[a * PASS : (a + 1) * PASS, b * PASS : (b + 1) * PASS]
+                nc.sync.dma_start(
+                    out=raw.rearrange("p (i r) -> p i r", i=PACK), in_=rows.rearrange("(p i) r -> p i r", i=PACK)
+                )
+                rounded = keep.tile([P, piece], BF16, name=f"even_bf{b}_{a}", align_bytes=64)
+                nc.vector.tensor_copy(
+                    out=rounded[:].rearrange("p (g u i) -> p g i u", u=4, i=PACK),
+                    in_=raw.rearrange("p (i g u) -> p g i u", i=PACK, u=4),
+                )
+                codes = keep.tile([P, PASS], U32, name=f"even_w{b}_{a}", align_bytes=64)
+                scales = keep.tile([P, PASS], U8, name=f"even_sc{b}_{a}", align_bytes=64)
+                nc.vector.quantize_mx(out=codes[:].bitcast(FP8X4), scales=scales[:], in_=rounded[:])
+                even_w[b, a], even_sc[b, a] = codes, scales
+
+        pool_w = keep.tile([P, H_PASSES, N], I32, name="pool_w", tag="words", align_bytes=64)
+        nc.sync.dma_start(out=pool_w[:], in_=w_pool_words.rearrange("b p c i -> p b (c i)").bitcast(I32))
+        gain = floats[:, H_PASSES * K_PASSES * piece :]
+        nc.sync.dma_start(out=gain, in_=wgo)
+
+        banks = [psum.tile([P, PASS], F32, name=f"bank{i}") for i in range(BANKS)]
+        used = []
+
+        def take_bank():
+            used.append(banks[len(used) % BANKS])
+            return used[-1]
+
+        squares, amp_w, amp_sc = {}, {}, {}
+
+        def respond(kind, c, b):
+            for jt in range(TILES):
+                cols = slice(jt * P, (jt + 1) * P)
+                sc_cols = slice(c % 2 * CHUNK + jt * P, c % 2 * CHUNK + (jt + 1) * P)
+                bank = take_bank()
+                for a in range(K_PASSES):
+                    if kind == "odd":
+                        moving = odd_w[:, a, 2 * b * PASS : 2 * (b + 1) * PASS].bitcast(FP4X4)
+                        moving_sc = odd_sc[:, a, b * PASS : (b + 1) * PASS]
+                        patch_sc = (picked_sc, second_sc)[a][c // 2][:, sc_cols]
+                    else:
+                        moving = even_w[b, a][:].bitcast(FP8X4)
+                        moving_sc = even_sc[b, a][:]
+                        patch_sc = picked_sc[c // 2][4 * a : P, sc_cols]
+                    nc.tensor.matmul_mx(
+                        out=bank[:],
+                        lhsT=patch_w[c, a][:, cols].bitcast(FP8X4),
+                        lhsT_scale=patch_sc,
+                        rhs=moving,
+                        rhs_scale=moving_sc,
+                        start=(a == 0),
+                        stop=(a == K_PASSES - 1),
+                    )
+                square = keep.tile([P, PACK, P], F32, name=f"{kind}_sq{c}_{b}_{jt}")
+                nc.scalar.activation(
+                    out=square[:], in_=bank[:].rearrange("p (m t) -> p t m", t=PACK), func=ACT.Square
+                )
+                squares[kind, c, b, jt] = [square]
+                if kind == "even" and c == 0:
+                    both = keep.tile([P, PACK, P], F32, name=f"both{c}_{b}_{jt}")
+                    nc.vector.tensor_tensor(both[:], squares["odd", c, b, jt][0][:], square[:], ADD)
+                    squares["odd", c, b, jt], squares["even", c, b, jt] = [], [both]
+
+        def amplitude(c, b):
+            amp = keep.tile([P, CHUNK * PACK], BF16, name=f"amp{c}_{b}", align_bytes=64)
+            for jt in range(TILES):
+                energy = take_bank()
+                terms = squares["odd", c, b, jt] + squares["even", c, b, jt]
+                for t in range(PACK):
+                    for i, term in enumerate(terms):
+                        nc.tensor.matmul(
+                            energy[:, t * P : (t + 1) * P],
+                            lhsT=term[:, t, :],
+                            rhs=ident[:],
+                            is_transpose=True,
+                            start=(i == 0),
+                            stop=(i == len(terms) - 1),
+                        )
+                nc.scalar.activation(
+                    out=amp[:, jt * PASS : (jt + 1) * PASS].rearrange("p (j t) -> p j t", t=PACK),
+                    in_=energy[:].rearrange("p (t j) -> p j t", t=PACK),
+                    func=ACT.Sqrt,
+                )
+            codes = keep.tile([P, CHUNK], U32, name=f"amp_w{c}_{b}", align_bytes=64)
+            scales = keep.tile([P, CHUNK], U8, name=f"amp_sc{c}_{b}", align_bytes=64)
+            nc.vector.quantize_mx(out=codes[:].bitcast(FP8X4), scales=scales[:], in_=amp[:])
+            amp_w[c, b], amp_sc[c, b] = codes, scales
+
+        def pool_and_place(c, n):
+            cols = slice(n * P, (n + 1) * P)
+            pooled = take_bank()[:, :CHUNK]
+            for b in range(H_PASSES):
+                nc.tensor.matmul_mx(
+                    out=pooled,
+                    lhsT=pool_w[:, b, cols].bitcast(FP8X4),
+                    lhsT_scale=pool_sc[4 * b : P, cols],
+                    rhs=amp_w[c, b][:].bitcast(FP8X4),
+                    rhs_scale=amp_sc[c, b][:],
+                    start=(b == 0),
+                    stop=(b == H_PASSES - 1),
+                )
+            y = keep.tile([P, CHUNK], F32, name=f"y{c}_{n}")
+            nc.scalar.copy(out=y[:], in_=pooled)
+            nc.vector.tensor_tensor(
+                pages[n][:].indirect(place_list[:, c * LIST_COLS : (c + 1) * LIST_COLS]),
+                y[:],
+                gain[:, c * CHUNK : (c + 1) * CHUNK],
+                MULT,
             )
 
         for c in range(CHUNKS):
-            if c + 3 - 1 < CHUNKS and c > 0:
-                patches.append(gather_patches(c + 3 - 1))
-            patch_w, patch_sc = patches[c]
-            amp_w, amp_sc = [], []
             for b in range(H_PASSES):
-                amp = keep.tile([P, CHUNK * PACK], BF16, name=f"amp{c}_{b}", align_bytes=64)
-                for jt in range(TILES):
-                    odd_sq = keep.tile([P, PACK, P], F32, name=f"odd_sq{c}_{b}_{jt}")
-                    squared_response(
-                        patch_w, patch_sc, jt, "odd_bank",
-                        [odd_w[a][:, 2 * b * PASS : 2 * (b + 1) * PASS].bitcast(FP4X4) for a in range(K_PASSES)],
-                        [odd_sc[:, a, b * PASS : (b + 1) * PASS] for a in range(K_PASSES)],
-                        odd_sq,
-                    )
-                    even_sq = ring.tile([P, PACK, P], F32, name="even_sq")
-                    squared_response(
-                        patch_w, patch_sc, jt, "even_bank",
-                        [even_w[b, a][:].bitcast(FP8X4) for a in range(K_PASSES)],
-                        [even_sc[b, a][:] for a in range(K_PASSES)],
-                        even_sq,
-                    )
-                    energy = psum.tile([P, PACK, P], F32, name="energy")
-                    if b == 0:
-                        both = ring.tile([P, PACK, P], F32, name="both")
-                        nc.vector.tensor_tensor(both[:], odd_sq[:], even_sq[:], ADD)
-                        for t in range(PACK):
-                            nc.tensor.transpose(energy[:, t, :], both[:, t, :], ident[:])
-                    else:
-                        for t in range(PACK):
-                            nc.tensor.matmul(energy[:, t, :], lhsT=odd_sq[:, t, :], rhs=ident[:], is_transpose=True, start=True, stop=False)
-                            nc.tensor.matmul(energy[:, t, :], lhsT=even_sq[:, t, :], rhs=ident[:], is_transpose=True, start=False, stop=True)
-                    nc.scalar.activation(
-                        out=amp[:, jt * PASS : (jt + 1) * PASS].rearrange("p (j t) -> p j t", t=PACK),
-                        in_=energy[:].rearrange("p t j -> p j t"),
-                        func=ACT.Sqrt,
-                    )
-                codes = keep.tile([P, CHUNK], U32, name=f"amp_w{c}_{b}", align_bytes=64)
-                scales = keep.tile([P, CHUNK], U8, name=f"amp_sc{c}_{b}", align_bytes=64)
-                nc.vector.quantize_mx(out=codes[:].bitcast(FP8X4), scales=scales[:], in_=amp[:])
-                amp_w.append(codes)
-                amp_sc.append(scales)
-
-            for n in range(PAGES):
-                cols = slice(n * P, (n + 1) * P)
-                pooled = psum.tile([P, CHUNK], F32, name="pooled")
-                for b in range(H_PASSES):
-                    nc.tensor.matmul_mx(
-                        out=pooled[:],
-                        lhsT=pool_w[:, b, cols].bitcast(FP8X4),
-                        lhsT_scale=pool_sc[4 * b : P, cols],
-                        rhs=amp_w[b][:].bitcast(FP8X4),
-                        rhs_scale=amp_sc[b][:],
-                        start=(b == 0),
-                        stop=(b == H_PASSES - 1),
-                    )
-                y = keep.tile([P, CHUNK], F32, name=f"y{c}_{n}")
-                nc.scalar.copy(out=y[:], in_=pooled[:])
-                nc.vector.tensor_tensor(
-                    pages[n][:].indirect(place_list[:, c * LIST_COLS : (c + 1) * LIST_COLS]),
-                    y[:],
-                    gain[:, c * CHUNK : (c + 1) * CHUNK],
-                    MULT,
-                )
+                respond("odd", c, b)
+        for c in range(CHUNKS):
+            respond("even", c, 0)
+            if c > 0:
+                pool_and_place(c - 1, 0)
+                pool_and_place(c - 1, 1)
+            respond("even", c, 1)
+            amplitude(c, 0)
+            amplitude(c, 1)
+            if c > 0:
+                pool_and_place(c - 1, 2)
+        for n in range(PAGES):
+            pool_and_place(CHUNKS - 1, n)
 
         for n in range(PAGES):
             nc.sync.dma_start(out=out[n * P : (n + 1) * P, :], in_=pages[n][:])

@@ -64,17 +64,6 @@ def tile_list_orientation_energy_store_kernel(
             )
         ident = keep.tile([P, P], F32, name="ident")
         make_identity(nc, ident[:])
-        pages = []
-        for n in range(PAGES):
-            page = keep.tile([P, T2], F32, name=f"page{n}")
-            nc.gpsimd.memset(page[:], 0.0)
-            pages.append(page)
-        pool_sc = keep.tile([P, N], U8, name="pool_sc", align_bytes=64)
-        nc.gpsimd.memset(pool_sc[:].bitcast(I32), 0)
-        for q in range(4):
-            nc.gpsimd.dma_start(
-                out=pool_sc[32 * q : 32 * q + 8, :].bitcast(I32), in_=w_pool_scales[:, 4 * q : 4 * q + 4, :].bitcast(I32)
-            )
 
         warm_in = keep.tile([P, 1], F32, name="warm_in")
         warm_out = keep.tile([P, 1], F32, name="warm_out")
@@ -90,6 +79,18 @@ def tile_list_orientation_energy_store_kernel(
             nc.scalar.dma_start(out=shifted[0 : P - 4, :].bitcast(I32), in_=picked[4:P, :].bitcast(I32))
             picked_sc.append(picked)
             second_sc.append(shifted)
+
+        pages = []
+        for n in range(PAGES):
+            page = keep.tile([P, T2], F32, name=f"page{n}")
+            (nc.vector if n < 2 else nc.gpsimd).memset(page[:], 0.0)
+            pages.append(page)
+        pool_sc = keep.tile([P, N], U8, name="pool_sc", align_bytes=64)
+        nc.gpsimd.memset(pool_sc[:].bitcast(I32), 0)
+        for q in range(4):
+            nc.gpsimd.dma_start(
+                out=pool_sc[32 * q : 32 * q + 8, :].bitcast(I32), in_=w_pool_scales[:, 4 * q : 4 * q + 4, :].bitcast(I32)
+            )
 
         patch_w = {}
         for c in range(CHUNKS):
@@ -163,7 +164,9 @@ def tile_list_orientation_energy_store_kernel(
                     )
                 square = keep.tile([P, PACK, P], F32, name=f"{kind}_sq{c}_{b}_{jt}")
                 nc.scalar.activation(
-                    out=square[:], in_=bank[:].rearrange("p (m t) -> p t m", t=PACK), func=ACT.Square
+                    out=square[:].rearrange("p t (g u) -> p g t u", u=4),
+                    in_=bank[:].rearrange("p (g u t) -> p g t u", u=4, t=PACK),
+                    func=ACT.Square,
                 )
                 squares[kind, c, b, jt] = [square]
                 if kind == "even" and c == 0:

@@ -45,9 +45,9 @@ def tile_list_orientation_energy_store_kernel(
         nc.sync.dma_start(place_list[:], offs2)
 
         tab_sc = keep.tile([P, T], U8, name="tab_sc", tag="scales_then_floats", align_bytes=64)
-        nc.vector.memset(tab_sc[:].bitcast(I32), 0)
+        nc.gpsimd.memset(tab_sc[:].bitcast(I32), 0)
         for q in range(4):
-            nc.scalar.dma_start(
+            (nc.scalar if q < 2 else nc.gpsimd).dma_start(
                 out=tab_sc[32 * q : 32 * q + 8, :].bitcast(I32), in_=tab_scales[:, 4 * q : 4 * q + 4, :].bitcast(I32)
             )
         tab_w = keep.tile([P, K_PASSES, T], I32, name="tab_w", tag="words", align_bytes=64)
@@ -56,7 +56,7 @@ def tile_list_orientation_energy_store_kernel(
         nc.sync.dma_start(out=odd_w[:].bitcast(I32), in_=w_odd_words.rearrange("a p c -> p a c").bitcast(I32))
 
         odd_sc = keep.tile([P, K_PASSES, H], U8, name="odd_sc", align_bytes=64)
-        nc.gpsimd.memset(odd_sc[:].bitcast(I32), 0)
+        nc.vector.memset(odd_sc[:].bitcast(I32), 0)
         for q in range(4):
             nc.gpsimd.dma_start(
                 out=odd_sc[32 * q : 32 * q + 4, :, :].bitcast(I32),
@@ -64,9 +64,14 @@ def tile_list_orientation_energy_store_kernel(
             )
         ident = keep.tile([P, P], F32, name="ident")
         make_identity(nc, ident[:])
+        pages = []
+        for n in range(PAGES):
+            page = keep.tile([P, T2], F32, name=f"page{n}")
+            nc.gpsimd.memset(page[:], 0.0)
+            pages.append(page)
 
         warm_in = keep.tile([P, 1], F32, name="warm_in")
-        warm_out = keep.tile([P, 1], F32, name="warm_out")
+        warm_out = keep.tile([P, 1], F32, name="warm_out", tag="warm_then_floats", align_bytes=64)
         nc.vector.memset(warm_in[:], 1.0)
         nc.scalar.activation(out=warm_out[:], in_=warm_in[:], func=ACT.Sqrt)
 
@@ -76,21 +81,13 @@ def tile_list_orientation_energy_store_kernel(
             nc.vector.memset(shifted[:].bitcast(I32), 0)
             picked = keep.tile([P, S // 2], U8, name=f"picked_sc{half}", align_bytes=64)
             nc.vector.tensor_copy(out=picked[:], in_=tab_sc[:].indirect(pick_list[:, half * 32 : (half + 1) * 32]))
-            nc.scalar.dma_start(out=shifted[0 : P - 4, :].bitcast(I32), in_=picked[4:P, :].bitcast(I32))
+            for first, rows in ((0, 64), (64, 32), (96, 4)):
+                nc.scalar.dma_start(
+                    out=shifted[first : first + rows, :].bitcast(I32),
+                    in_=picked[first + 4 : first + 4 + rows, :].bitcast(I32),
+                )
             picked_sc.append(picked)
             second_sc.append(shifted)
-
-        pages = []
-        for n in range(PAGES):
-            page = keep.tile([P, T2], F32, name=f"page{n}")
-            (nc.vector if n < 2 else nc.gpsimd).memset(page[:], 0.0)
-            pages.append(page)
-        pool_sc = keep.tile([P, N], U8, name="pool_sc", align_bytes=64)
-        nc.gpsimd.memset(pool_sc[:].bitcast(I32), 0)
-        for q in range(4):
-            nc.gpsimd.dma_start(
-                out=pool_sc[32 * q : 32 * q + 8, :].bitcast(I32), in_=w_pool_scales[:, 4 * q : 4 * q + 4, :].bitcast(I32)
-            )
 
         patch_w = {}
         for c in range(CHUNKS):
@@ -103,19 +100,19 @@ def tile_list_orientation_energy_store_kernel(
                 patch_w[c, a] = picked
 
         piece = PACK * PASS
-        floats = keep.tile(
-            [P, H_PASSES * K_PASSES * piece + S], F32, name="floats", tag="scales_then_floats", align_bytes=64
-        )
+        floats = [
+            keep.tile([P, K_PASSES * piece], F32, name="floats0", tag="warm_then_floats", align_bytes=64),
+            keep.tile([P, K_PASSES * piece + S], F32, name="floats1", tag="scales_then_floats", align_bytes=64),
+        ]
         even_w, even_sc = {}, {}
         for b in range(H_PASSES):
             for a in range(K_PASSES):
-                first = (b * K_PASSES + a) * piece
-                raw = floats[:, first : first + piece]
+                raw = floats[b][:, a * piece : (a + 1) * piece]
                 rows = w_even[a * PASS : (a + 1) * PASS, b * PASS : (b + 1) * PASS]
                 nc.sync.dma_start(
                     out=raw.rearrange("p (i r) -> p i r", i=PACK), in_=rows.rearrange("(p i) r -> p i r", i=PACK)
                 )
-                rounded = keep.tile([P, piece], BF16, name=f"even_bf{b}_{a}", align_bytes=64)
+                rounded = keep.tile([P, piece], BF16, name=f"even_bf{b}_{a}", tag=f"rounded{b}_{a}", align_bytes=64)
                 nc.vector.tensor_copy(
                     out=rounded[:].rearrange("p (g u i) -> p g i u", u=4, i=PACK),
                     in_=raw.rearrange("p (i g u) -> p g i u", i=PACK, u=4),
@@ -127,7 +124,13 @@ def tile_list_orientation_energy_store_kernel(
 
         pool_w = keep.tile([P, H_PASSES, N], I32, name="pool_w", tag="words", align_bytes=64)
         nc.sync.dma_start(out=pool_w[:], in_=w_pool_words.rearrange("b p c i -> p b (c i)").bitcast(I32))
-        gain = floats[:, H_PASSES * K_PASSES * piece :]
+        pool_sc = keep.tile([P, N], U8, name="pool_sc", tag="rounded0_0", align_bytes=64)
+        nc.vector.memset(pool_sc[:].bitcast(I32), 0)
+        for q in range(4):
+            nc.sync.dma_start(
+                out=pool_sc[32 * q : 32 * q + 8, :].bitcast(I32), in_=w_pool_scales[:, 4 * q : 4 * q + 4, :].bitcast(I32)
+            )
+        gain = floats[1][:, K_PASSES * piece :]
         nc.sync.dma_start(out=gain, in_=wgo)
 
         banks = [psum.tile([P, PASS], F32, name=f"bank{i}") for i in range(BANKS)]
@@ -169,7 +172,7 @@ def tile_list_orientation_energy_store_kernel(
                     func=ACT.Square,
                 )
                 squares[kind, c, b, jt] = [square]
-                if kind == "even" and c == 0:
+                if kind == "even" and c == 1:
                     both = keep.tile([P, PACK, P], F32, name=f"both{c}_{b}_{jt}")
                     nc.vector.tensor_tensor(both[:], squares["odd", c, b, jt][0][:], square[:], ADD)
                     squares["odd", c, b, jt], squares["even", c, b, jt] = [], [both]
@@ -199,6 +202,10 @@ def tile_list_orientation_energy_store_kernel(
             nc.vector.quantize_mx(out=codes[:].bitcast(FP8X4), scales=scales[:], in_=amp[:])
             amp_w[c, b], amp_sc[c, b] = codes, scales
 
+        def amplitudes(c):
+            for b in range(H_PASSES):
+                amplitude(c, b)
+
         def pool_and_place(c, n):
             cols = slice(n * P, (n + 1) * P)
             pooled = take_bank()[:, :CHUNK]
@@ -221,21 +228,23 @@ def tile_list_orientation_energy_store_kernel(
                 MULT,
             )
 
-        for c in range(CHUNKS):
-            for b in range(H_PASSES):
-                respond("odd", c, b)
-        for c in range(CHUNKS):
-            respond("even", c, 0)
-            if c > 0:
-                pool_and_place(c - 1, 0)
-                pool_and_place(c - 1, 1)
-            respond("even", c, 1)
-            amplitude(c, 0)
-            amplitude(c, 1)
-            if c > 0:
-                pool_and_place(c - 1, 2)
-        for n in range(PAGES):
-            pool_and_place(CHUNKS - 1, n)
+        pairs = [(c, b) for c in range(CHUNKS) for b in range(H_PASSES)]
+        for c, b in pairs[:-1]:
+            respond("odd", c, b)
+        respond("even", 0, 0)
+        respond("even", 1, 0)
+        respond("even", 0, 1)
+        amplitudes(0)
+        later = [lambda: respond("even", 1, 1), lambda: respond("odd", *pairs[-1]), lambda: amplitudes(1)]
+        for c in range(2, CHUNKS):
+            later.extend([lambda c=c, b=b: respond("even", c, b) for b in range(H_PASSES)])
+            later.append(lambda c=c: amplitudes(c))
+        tasks = [(c, n) for c in range(CHUNKS) for n in range(PAGES)]
+        for step, (c, n) in zip(later, tasks):
+            step()
+            pool_and_place(c, n)
+        for c, n in tasks[len(later) :]:
+            pool_and_place(c, n)
 
         for n in range(PAGES):
             nc.sync.dma_start(out=out[n * P : (n + 1) * P, :], in_=pages[n][:])

@@ -1,7 +1,6 @@
 from contextlib import ExitStack
 
 import concourse.mybir as mybir
-from concourse.masks import make_identity
 
 K, H, N, T, S, T2 = 1024, 1024, 384, 2048, 1024, 2048
 FLOPS = 2 * 2 * K * H * S + 2 * H * N * S
@@ -29,6 +28,7 @@ TILES = CHUNK // P
 PAGES = N // P
 LIST_COLS = CHUNK // 16
 BANKS = 8
+VECTOR_SUMS = ((1, 0), (1, 1),)
 
 
 def tile_list_orientation_energy_store_kernel(
@@ -37,33 +37,54 @@ def tile_list_orientation_energy_store_kernel(
     nc = tc.nc
     with ExitStack() as ctx:
         keep = ctx.enter_context(tc.tile_pool(name="keep", bufs=1))
+        reuse = ctx.enter_context(tc.tile_pool(name="reuse", bufs=1))
         psum = ctx.enter_context(tc.psum_pool(name="psum", bufs=1))
 
         pick_list = keep.tile([P, S // 16], U16, name="pick_list")
         nc.sync.dma_start(pick_list[:], offs)
         place_list = keep.tile([P, S // 16], U16, name="place_list")
         nc.sync.dma_start(place_list[:], offs2)
-
-        tab_sc = keep.tile([P, T], U8, name="tab_sc", tag="scales_then_floats", align_bytes=64)
-        nc.gpsimd.memset(tab_sc[:].bitcast(I32), 0)
-        for q in range(4):
-            (nc.scalar if q < 2 else nc.gpsimd).dma_start(
-                out=tab_sc[32 * q : 32 * q + 8, :].bitcast(I32), in_=tab_scales[:, 4 * q : 4 * q + 4, :].bitcast(I32)
-            )
-        tab_w = keep.tile([P, K_PASSES, T], I32, name="tab_w", tag="words", align_bytes=64)
-        nc.sync.dma_start(out=tab_w[:], in_=tab_words.rearrange("a p t i -> p a (t i)").bitcast(I32))
         odd_w = keep.tile([P, K_PASSES, 2 * H], U8, name="odd_w", align_bytes=64)
         nc.sync.dma_start(out=odd_w[:].bitcast(I32), in_=w_odd_words.rearrange("a p c -> p a c").bitcast(I32))
 
-        odd_sc = keep.tile([P, K_PASSES, H], U8, name="odd_sc", align_bytes=64)
-        nc.vector.memset(odd_sc[:].bitcast(I32), 0)
+        piece = PACK * PASS
+        table_bytes = K_PASSES * T * 4
+        float_cols = H_PASSES * K_PASSES * piece + S
+        ident = keep.tile([P, P], F32, name="ident")
+        zeros = reuse.tile([P, P], F32, name="zeros", offset=table_bytes - 2 * P)
+        nc.gpsimd.memset(zeros[:], 0.0)
+        tab_sc = keep.tile([P, K_PASSES * T], U8, name="tab_sc", align_bytes=64)
+        nc.gpsimd.memset(tab_sc[:].bitcast(I32), 0)
         for q in range(4):
-            nc.gpsimd.dma_start(
+            nc.sync.dma_start(
+                out=tab_sc[32 * q : 32 * q + 4, :].bitcast(I32).rearrange("r (a t) -> r a t", a=K_PASSES),
+                in_=tab_scales[:, 4 * q : 4 * q + 4, :].rearrange("a r t -> r a t").bitcast(I32),
+            )
+
+        nc.gpsimd.affine_select(
+            out=ident[:],
+            in_=zeros[:],
+            compare_op=mybir.AluOpType.not_equal,
+            fill=1.0,
+            base=0,
+            pattern=[[-1, P]],
+            channel_multiplier=1,
+        )
+        tab_w = reuse.tile([P, K_PASSES * T], I32, name="tab_w", align_bytes=64, offset=0)
+        floats = reuse.tile([P, float_cols], F32, name="floats", align_bytes=64, offset=table_bytes)
+        last_at = table_bytes + 4 * float_cols
+        nc.sync.dma_start(
+            out=tab_w[:].rearrange("p (a t) -> p a t", a=K_PASSES),
+            in_=tab_words.rearrange("a p t i -> p a (t i)").bitcast(I32),
+        )
+
+        odd_sc = keep.tile([P, K_PASSES, H], U8, name="odd_sc", align_bytes=64)
+        nc.gpsimd.memset(odd_sc[:].bitcast(I32), 0)
+        for q in range(4):
+            nc.scalar.dma_start(
                 out=odd_sc[32 * q : 32 * q + 4, :, :].bitcast(I32),
                 in_=w_odd_scales[:, 4 * q : 4 * q + 4, :].rearrange("a r c -> r a c").bitcast(I32),
             )
-        ident = keep.tile([P, P], F32, name="ident")
-        make_identity(nc, ident[:])
         pages = []
         for n in range(PAGES):
             page = keep.tile([P, T2], F32, name=f"page{n}")
@@ -71,48 +92,46 @@ def tile_list_orientation_energy_store_kernel(
             pages.append(page)
 
         warm_in = keep.tile([P, 1], F32, name="warm_in")
-        warm_out = keep.tile([P, 1], F32, name="warm_out", tag="warm_then_floats", align_bytes=64)
+        warm_out = keep.tile([P, 1], F32, name="warm_out")
         nc.vector.memset(warm_in[:], 1.0)
         nc.scalar.activation(out=warm_out[:], in_=warm_in[:], func=ACT.Sqrt)
 
-        picked_sc, second_sc = [], []
-        for half in range(2):
-            shifted = keep.tile([P, S // 2], U8, name=f"second_sc{half}", align_bytes=64)
-            nc.vector.memset(shifted[:].bitcast(I32), 0)
-            picked = keep.tile([P, S // 2], U8, name=f"picked_sc{half}", align_bytes=64)
-            nc.vector.tensor_copy(out=picked[:], in_=tab_sc[:].indirect(pick_list[:, half * 32 : (half + 1) * 32]))
-            for first, rows in ((0, 64), (64, 32), (96, 4)):
-                nc.scalar.dma_start(
-                    out=shifted[first : first + rows, :].bitcast(I32),
-                    in_=picked[first + 4 : first + 4 + rows, :].bitcast(I32),
-                )
-            picked_sc.append(picked)
-            second_sc.append(shifted)
+        patch_w, patch_sc = {}, {}
 
-        patch_w = {}
+        def pick_scales(c, a, pool, offset=None):
+            picked = pool.tile([P, CHUNK], U8, name=f"patch_sc{c}_{a}", align_bytes=64, offset=offset)
+            nc.vector.tensor_copy(
+                out=picked[:],
+                in_=tab_sc[:, a * T : (a + 1) * T].indirect(pick_list[:, c * LIST_COLS : (c + 1) * LIST_COLS]),
+            )
+            patch_sc[c, a] = picked
+
+        def pick_words(c, a, pool, offset=None):
+            picked = pool.tile([P, CHUNK], U32, name=f"patch_w{c}_{a}", align_bytes=64, offset=offset)
+            nc.vector.tensor_copy(
+                out=picked[:],
+                in_=tab_w[:, a * T : (a + 1) * T].bitcast(U32).indirect(pick_list[:, c * LIST_COLS : (c + 1) * LIST_COLS]),
+            )
+            patch_w[c, a] = picked
+
         for c in range(CHUNKS):
             for a in range(K_PASSES):
-                picked = keep.tile([P, CHUNK], U32, name=f"patch_w{c}_{a}", align_bytes=64)
-                nc.vector.tensor_copy(
-                    out=picked[:],
-                    in_=tab_w[:, a, :].bitcast(U32).indirect(pick_list[:, c * LIST_COLS : (c + 1) * LIST_COLS]),
-                )
-                patch_w[c, a] = picked
+                pick_scales(c, a, keep)
+                if c < CHUNKS - 1:
+                    pick_words(c, a, keep)
 
-        piece = PACK * PASS
-        floats = [
-            keep.tile([P, K_PASSES * piece], F32, name="floats0", tag="warm_then_floats", align_bytes=64),
-            keep.tile([P, K_PASSES * piece + S], F32, name="floats1", tag="scales_then_floats", align_bytes=64),
-        ]
         even_w, even_sc = {}, {}
         for b in range(H_PASSES):
             for a in range(K_PASSES):
-                raw = floats[b][:, a * piece : (a + 1) * piece]
+                raw = floats[:, (b * K_PASSES + a) * piece : (b * K_PASSES + a + 1) * piece]
                 rows = w_even[a * PASS : (a + 1) * PASS, b * PASS : (b + 1) * PASS]
                 nc.sync.dma_start(
                     out=raw.rearrange("p (i r) -> p i r", i=PACK), in_=rows.rearrange("(p i) r -> p i r", i=PACK)
                 )
-                rounded = keep.tile([P, piece], BF16, name=f"even_bf{b}_{a}", tag=f"rounded{b}_{a}", align_bytes=64)
+                if (b, a) == (H_PASSES - 1, K_PASSES - 1):
+                    rounded = reuse.tile([P, piece], BF16, name="even_bf_last", align_bytes=64, offset=last_at)
+                else:
+                    rounded = keep.tile([P, piece], BF16, name=f"even_bf{b}_{a}", tag=f"rounded{b}_{a}", align_bytes=64)
                 nc.vector.tensor_copy(
                     out=rounded[:].rearrange("p (g u i) -> p g i u", u=4, i=PACK),
                     in_=raw.rearrange("p (i g u) -> p g i u", i=PACK, u=4),
@@ -122,16 +141,19 @@ def tile_list_orientation_energy_store_kernel(
                 nc.vector.quantize_mx(out=codes[:].bitcast(FP8X4), scales=scales[:], in_=rounded[:])
                 even_w[b, a], even_sc[b, a] = codes, scales
 
-        pool_w = keep.tile([P, H_PASSES, N], I32, name="pool_w", tag="words", align_bytes=64)
+        for a in range(K_PASSES):
+            pick_words(CHUNKS - 1, a, reuse, offset=last_at + a * 5 * CHUNK + CHUNK)
+
+        gain = floats[:, H_PASSES * K_PASSES * piece :]
+        nc.sync.dma_start(out=gain, in_=wgo)
+        pool_w = keep.tile([P, H_PASSES, N], I32, name="pool_w", tag="rounded0_0", align_bytes=64)
         nc.sync.dma_start(out=pool_w[:], in_=w_pool_words.rearrange("b p c i -> p b (c i)").bitcast(I32))
-        pool_sc = keep.tile([P, N], U8, name="pool_sc", tag="rounded0_0", align_bytes=64)
+        pool_sc = keep.tile([P, N], U8, name="pool_sc", tag="rounded0_1", align_bytes=64)
         nc.vector.memset(pool_sc[:].bitcast(I32), 0)
         for q in range(4):
             nc.sync.dma_start(
                 out=pool_sc[32 * q : 32 * q + 8, :].bitcast(I32), in_=w_pool_scales[:, 4 * q : 4 * q + 4, :].bitcast(I32)
             )
-        gain = floats[1][:, K_PASSES * piece :]
-        nc.sync.dma_start(out=gain, in_=wgo)
 
         banks = [psum.tile([P, PASS], F32, name=f"bank{i}") for i in range(BANKS)]
         used = []
@@ -142,40 +164,43 @@ def tile_list_orientation_energy_store_kernel(
 
         squares, amp_w, amp_sc = {}, {}, {}
 
+        def response_pass(kind, c, b, jt, a, bank):
+            cols = slice(jt * P, (jt + 1) * P)
+            if kind == "odd":
+                moving = odd_w[:, a, 2 * b * PASS : 2 * (b + 1) * PASS].bitcast(FP4X4)
+                moving_sc = odd_sc[:, a, b * PASS : (b + 1) * PASS]
+            else:
+                moving = even_w[b, a][:].bitcast(FP8X4)
+                moving_sc = even_sc[b, a][:]
+            nc.tensor.matmul_mx(
+                out=bank[:],
+                lhsT=patch_w[c, a][:, cols].bitcast(FP8X4),
+                lhsT_scale=patch_sc[c, a][:, cols],
+                rhs=moving,
+                rhs_scale=moving_sc,
+                start=(a == 0),
+                stop=(a == K_PASSES - 1),
+            )
+
+        def square_bank(kind, c, b, jt, bank):
+            square = keep.tile([P, PACK, P], F32, name=f"{kind}_sq{c}_{b}_{jt}")
+            nc.scalar.activation(
+                out=square[:].rearrange("p t (g u) -> p g t u", u=4),
+                in_=bank[:].rearrange("p (g u t) -> p g t u", u=4, t=PACK),
+                func=ACT.Square,
+            )
+            squares[kind, c, b, jt] = [square]
+            if kind == "even" and (c, b) in VECTOR_SUMS:
+                both = keep.tile([P, PACK, P], F32, name=f"both{c}_{b}_{jt}")
+                nc.vector.tensor_tensor(both[:], squares["odd", c, b, jt][0][:], square[:], ADD)
+                squares["odd", c, b, jt], squares["even", c, b, jt] = [], [both]
+
         def respond(kind, c, b):
             for jt in range(TILES):
-                cols = slice(jt * P, (jt + 1) * P)
-                sc_cols = slice(c % 2 * CHUNK + jt * P, c % 2 * CHUNK + (jt + 1) * P)
                 bank = take_bank()
                 for a in range(K_PASSES):
-                    if kind == "odd":
-                        moving = odd_w[:, a, 2 * b * PASS : 2 * (b + 1) * PASS].bitcast(FP4X4)
-                        moving_sc = odd_sc[:, a, b * PASS : (b + 1) * PASS]
-                        patch_sc = (picked_sc, second_sc)[a][c // 2][:, sc_cols]
-                    else:
-                        moving = even_w[b, a][:].bitcast(FP8X4)
-                        moving_sc = even_sc[b, a][:]
-                        patch_sc = picked_sc[c // 2][4 * a : P, sc_cols]
-                    nc.tensor.matmul_mx(
-                        out=bank[:],
-                        lhsT=patch_w[c, a][:, cols].bitcast(FP8X4),
-                        lhsT_scale=patch_sc,
-                        rhs=moving,
-                        rhs_scale=moving_sc,
-                        start=(a == 0),
-                        stop=(a == K_PASSES - 1),
-                    )
-                square = keep.tile([P, PACK, P], F32, name=f"{kind}_sq{c}_{b}_{jt}")
-                nc.scalar.activation(
-                    out=square[:].rearrange("p t (g u) -> p g t u", u=4),
-                    in_=bank[:].rearrange("p (g u t) -> p g t u", u=4, t=PACK),
-                    func=ACT.Square,
-                )
-                squares[kind, c, b, jt] = [square]
-                if kind == "even" and c == 1:
-                    both = keep.tile([P, PACK, P], F32, name=f"both{c}_{b}_{jt}")
-                    nc.vector.tensor_tensor(both[:], squares["odd", c, b, jt][0][:], square[:], ADD)
-                    squares["odd", c, b, jt], squares["even", c, b, jt] = [], [both]
+                    response_pass(kind, c, b, jt, a, bank)
+                square_bank(kind, c, b, jt, bank)
 
         def amplitude(c, b):
             amp = keep.tile([P, CHUNK * PACK], BF16, name=f"amp{c}_{b}", align_bytes=64)
@@ -202,10 +227,6 @@ def tile_list_orientation_energy_store_kernel(
             nc.vector.quantize_mx(out=codes[:].bitcast(FP8X4), scales=scales[:], in_=amp[:])
             amp_w[c, b], amp_sc[c, b] = codes, scales
 
-        def amplitudes(c):
-            for b in range(H_PASSES):
-                amplitude(c, b)
-
         def pool_and_place(c, n):
             cols = slice(n * P, (n + 1) * P)
             pooled = take_bank()[:, :CHUNK]
@@ -228,23 +249,41 @@ def tile_list_orientation_energy_store_kernel(
                 MULT,
             )
 
-        pairs = [(c, b) for c in range(CHUNKS) for b in range(H_PASSES)]
-        for c, b in pairs[:-1]:
-            respond("odd", c, b)
+        respond("odd", 0, 0)
+        respond("odd", 0, 1)
+        respond("odd", 1, 0)
+        respond("odd", 1, 1)
+        respond("odd", 2, 0)
+        respond("odd", 2, 1)
         respond("even", 0, 0)
         respond("even", 1, 0)
         respond("even", 0, 1)
-        amplitudes(0)
-        later = [lambda: respond("even", 1, 1), lambda: respond("odd", *pairs[-1]), lambda: amplitudes(1)]
-        for c in range(2, CHUNKS):
-            later.extend([lambda c=c, b=b: respond("even", c, b) for b in range(H_PASSES)])
-            later.append(lambda c=c: amplitudes(c))
-        tasks = [(c, n) for c in range(CHUNKS) for n in range(PAGES)]
-        for step, (c, n) in zip(later, tasks):
-            step()
-            pool_and_place(c, n)
-        for c, n in tasks[len(later) :]:
-            pool_and_place(c, n)
-
+        amplitude(0, 0)
+        amplitude(0, 1)
+        respond("even", 1, 1)
+        pool_and_place(0, 0)
+        respond("odd", 3, 0)
+        pool_and_place(0, 1)
+        respond("odd", 3, 1)
+        amplitude(1, 0)
+        amplitude(1, 1)
+        pool_and_place(0, 2)
+        respond("even", 2, 0)
+        pool_and_place(1, 0)
+        respond("even", 2, 1)
+        pool_and_place(1, 1)
+        amplitude(2, 0)
+        amplitude(2, 1)
+        pool_and_place(1, 2)
+        respond("even", 3, 0)
+        pool_and_place(2, 0)
+        respond("even", 3, 1)
+        pool_and_place(2, 1)
+        amplitude(3, 0)
+        amplitude(3, 1)
+        pool_and_place(2, 2)
+        pool_and_place(3, 0)
+        pool_and_place(3, 1)
+        pool_and_place(3, 2)
         for n in range(PAGES):
             nc.sync.dma_start(out=out[n * P : (n + 1) * P, :], in_=pages[n][:])

@@ -28,7 +28,7 @@ TILES = CHUNK // P
 PAGES = N // P
 LIST_COLS = CHUNK // 16
 BANKS = 8
-VECTOR_SUMS = ((1, 0), (1, 1),)
+VECTOR_SUMS = ((1, 0), (0, 1), (1, 1),)
 
 
 def tile_list_orientation_energy_store_kernel(
@@ -257,29 +257,29 @@ def tile_list_orientation_energy_store_kernel(
         respond("odd", 2, 1)
         respond("even", 0, 0)
         respond("even", 1, 0)
-        respond("even", 0, 1)
         amplitude(0, 0)
+        respond("even", 0, 1)
+        amplitude(1, 0)
         amplitude(0, 1)
         respond("even", 1, 1)
-        pool_and_place(0, 0)
         respond("odd", 3, 0)
-        pool_and_place(0, 1)
-        respond("odd", 3, 1)
-        amplitude(1, 0)
+        pool_and_place(0, 0)
         amplitude(1, 1)
-        pool_and_place(0, 2)
+        respond("odd", 3, 1)
+        pool_and_place(0, 1)
         respond("even", 2, 0)
-        pool_and_place(1, 0)
+        pool_and_place(0, 2)
         respond("even", 2, 1)
-        pool_and_place(1, 1)
+        pool_and_place(1, 0)
         amplitude(2, 0)
+        pool_and_place(1, 1)
+        respond("even", 3, 0)
         amplitude(2, 1)
         pool_and_place(1, 2)
-        respond("even", 3, 0)
-        pool_and_place(2, 0)
         respond("even", 3, 1)
-        pool_and_place(2, 1)
+        pool_and_place(2, 0)
         amplitude(3, 0)
+        pool_and_place(2, 1)
         amplitude(3, 1)
         pool_and_place(2, 2)
         pool_and_place(3, 0)

@@ -1,6 +1,7 @@
 from contextlib import ExitStack
 
 import concourse.mybir as mybir
+from concourse.masks import make_identity
 
 K, H, N, T, S, T2 = 1024, 1024, 384, 2048, 1024, 2048
 FLOPS = 2 * 2 * K * H * S + 2 * H * N * S
@@ -28,7 +29,7 @@ TILES = CHUNK // P
 PAGES = N // P
 LIST_COLS = CHUNK // 16
 BANKS = 8
-VECTOR_SUMS = ((1, 0), (0, 1), (1, 1),)
+VECTOR_SUMS = ((1, 1), (2, 0),)
 
 
 def tile_list_orientation_energy_store_kernel(
@@ -42,17 +43,11 @@ def tile_list_orientation_energy_store_kernel(
 
         pick_list = keep.tile([P, S // 16], U16, name="pick_list")
         nc.sync.dma_start(pick_list[:], offs)
-        place_list = keep.tile([P, S // 16], U16, name="place_list")
-        nc.sync.dma_start(place_list[:], offs2)
-        odd_w = keep.tile([P, K_PASSES, 2 * H], U8, name="odd_w", align_bytes=64)
-        nc.sync.dma_start(out=odd_w[:].bitcast(I32), in_=w_odd_words.rearrange("a p c -> p a c").bitcast(I32))
 
         piece = PACK * PASS
-        table_bytes = K_PASSES * T * 4
-        float_cols = H_PASSES * K_PASSES * piece + S
-        ident = keep.tile([P, P], F32, name="ident")
-        zeros = reuse.tile([P, P], F32, name="zeros", offset=table_bytes - 2 * P)
-        nc.gpsimd.memset(zeros[:], 0.0)
+        tab_w = keep.tile([P, K_PASSES * T], I32, name="tab_w", align_bytes=64)
+        nc.sync.dma_start(out=tab_w[:, :T], in_=tab_words[0].rearrange("p t i -> p (t i)").bitcast(I32))
+
         tab_sc = keep.tile([P, K_PASSES * T], U8, name="tab_sc", align_bytes=64)
         nc.gpsimd.memset(tab_sc[:].bitcast(I32), 0)
         for q in range(4):
@@ -60,31 +55,27 @@ def tile_list_orientation_energy_store_kernel(
                 out=tab_sc[32 * q : 32 * q + 4, :].bitcast(I32).rearrange("r (a t) -> r a t", a=K_PASSES),
                 in_=tab_scales[:, 4 * q : 4 * q + 4, :].rearrange("a r t -> r a t").bitcast(I32),
             )
+        odd_w = [keep.tile([P, K_PASSES, 2 * PASS], U8, name=f"odd_w{b}", align_bytes=64) for b in range(H_PASSES)]
 
-        nc.gpsimd.affine_select(
-            out=ident[:],
-            in_=zeros[:],
-            compare_op=mybir.AluOpType.not_equal,
-            fill=1.0,
-            base=0,
-            pattern=[[-1, P]],
-            channel_multiplier=1,
-        )
-        tab_w = reuse.tile([P, K_PASSES * T], I32, name="tab_w", align_bytes=64, offset=0)
-        floats = reuse.tile([P, float_cols], F32, name="floats", align_bytes=64, offset=table_bytes)
-        last_at = table_bytes + 4 * float_cols
-        nc.sync.dma_start(
-            out=tab_w[:].rearrange("p (a t) -> p a t", a=K_PASSES),
-            in_=tab_words.rearrange("a p t i -> p a (t i)").bitcast(I32),
-        )
+        def load_odd_words(b):
+            nc.sync.dma_start(
+                out=odd_w[b][:].bitcast(I32),
+                in_=w_odd_words[:, :, 2 * b * PASS : 2 * (b + 1) * PASS].rearrange("a p c -> p a c").bitcast(I32),
+            )
 
+        load_odd_words(0)
         odd_sc = keep.tile([P, K_PASSES, H], U8, name="odd_sc", align_bytes=64)
         nc.gpsimd.memset(odd_sc[:].bitcast(I32), 0)
         for q in range(4):
-            nc.scalar.dma_start(
+            nc.sync.dma_start(
                 out=odd_sc[32 * q : 32 * q + 4, :, :].bitcast(I32),
                 in_=w_odd_scales[:, 4 * q : 4 * q + 4, :].rearrange("a r c -> r a c").bitcast(I32),
             )
+        nc.sync.dma_start(out=tab_w[:, T:], in_=tab_words[1].rearrange("p t i -> p (t i)").bitcast(I32))
+        load_odd_words(1)
+
+        ident = keep.tile([P, P], F32, name="ident")
+        make_identity(nc, ident[:])
         pages = []
         for n in range(PAGES):
             page = keep.tile([P, T2], F32, name=f"page{n}")
@@ -114,27 +105,33 @@ def tile_list_orientation_energy_store_kernel(
             )
             patch_w[c, a] = picked
 
-        for c in range(CHUNKS):
-            for a in range(K_PASSES):
+        for a in range(K_PASSES):
+            for c in range(2):
                 pick_scales(c, a, keep)
-                if c < CHUNKS - 1:
-                    pick_words(c, a, keep)
+            for c in range(2):
+                pick_words(c, a, keep)
+        late_w = keep.tile([P, 2 * CHUNK], U32, name="late_w", align_bytes=64)
+        nc.vector.tensor_copy(out=late_w[:], in_=tab_w[:].bitcast(U32).indirect(pick_list[:, 2 * LIST_COLS :]))
+        patch_w[2, 0], patch_w[3, 0] = late_w[:, :CHUNK], late_w[:, CHUNK:]
+        for a in range(K_PASSES):
+            pick_scales(2, a, keep)
+        pick_words(2, 1, keep)
 
         even_w, even_sc = {}, {}
         for b in range(H_PASSES):
             for a in range(K_PASSES):
-                raw = floats[:, (b * K_PASSES + a) * piece : (b * K_PASSES + a + 1) * piece]
+                raw = keep.tile([P, piece], F32, name=f"even_raw{b}_{a}")
                 rows = w_even[a * PASS : (a + 1) * PASS, b * PASS : (b + 1) * PASS]
                 nc.sync.dma_start(
-                    out=raw.rearrange("p (i r) -> p i r", i=PACK), in_=rows.rearrange("(p i) r -> p i r", i=PACK)
+                    out=raw[:].rearrange("p (i r) -> p i r", i=PACK), in_=rows.rearrange("(p i) r -> p i r", i=PACK)
                 )
                 if (b, a) == (H_PASSES - 1, K_PASSES - 1):
-                    rounded = reuse.tile([P, piece], BF16, name="even_bf_last", align_bytes=64, offset=last_at)
+                    rounded = reuse.tile([P, piece], BF16, name="even_bf_last", align_bytes=64, offset=0)
                 else:
                     rounded = keep.tile([P, piece], BF16, name=f"even_bf{b}_{a}", tag=f"rounded{b}_{a}", align_bytes=64)
                 nc.vector.tensor_copy(
                     out=rounded[:].rearrange("p (g u i) -> p g i u", u=4, i=PACK),
-                    in_=raw.rearrange("p (i g u) -> p g i u", i=PACK, u=4),
+                    in_=raw[:].rearrange("p (i g u) -> p g i u", i=PACK, u=4),
                 )
                 codes = keep.tile([P, PASS], U32, name=f"even_w{b}_{a}", align_bytes=64)
                 scales = keep.tile([P, PASS], U8, name=f"even_sc{b}_{a}", align_bytes=64)
@@ -142,14 +139,17 @@ def tile_list_orientation_energy_store_kernel(
                 even_w[b, a], even_sc[b, a] = codes, scales
 
         for a in range(K_PASSES):
-            pick_words(CHUNKS - 1, a, reuse, offset=last_at + a * 5 * CHUNK + CHUNK)
+            pick_scales(CHUNKS - 1, a, reuse, offset=a * 5 * CHUNK)
+        pick_words(CHUNKS - 1, 1, reuse, offset=CHUNK)
 
-        gain = floats[:, H_PASSES * K_PASSES * piece :]
-        nc.sync.dma_start(out=gain, in_=wgo)
-        pool_w = keep.tile([P, H_PASSES, N], I32, name="pool_w", tag="rounded0_0", align_bytes=64)
+        gain = keep.tile([P, S], F32, name="gain")
+        nc.sync.dma_start(out=gain[:], in_=wgo)
+        place_list = keep.tile([P, S // 16], U16, name="place_list")
+        nc.sync.dma_start(place_list[:], offs2)
+        pool_w = keep.tile([P, H_PASSES, N], I32, name="pool_w", align_bytes=64)
         nc.sync.dma_start(out=pool_w[:], in_=w_pool_words.rearrange("b p c i -> p b (c i)").bitcast(I32))
-        pool_sc = keep.tile([P, N], U8, name="pool_sc", tag="rounded0_1", align_bytes=64)
-        nc.vector.memset(pool_sc[:].bitcast(I32), 0)
+        pool_sc = keep.tile([P, N], U8, name="pool_sc", align_bytes=64)
+        nc.gpsimd.memset(pool_sc[:].bitcast(I32), 0)
         for q in range(4):
             nc.sync.dma_start(
                 out=pool_sc[32 * q : 32 * q + 8, :].bitcast(I32), in_=w_pool_scales[:, 4 * q : 4 * q + 4, :].bitcast(I32)
@@ -167,7 +167,7 @@ def tile_list_orientation_energy_store_kernel(
         def response_pass(kind, c, b, jt, a, bank):
             cols = slice(jt * P, (jt + 1) * P)
             if kind == "odd":
-                moving = odd_w[:, a, 2 * b * PASS : 2 * (b + 1) * PASS].bitcast(FP4X4)
+                moving = odd_w[b][:, a, :].bitcast(FP4X4)
                 moving_sc = odd_sc[:, a, b * PASS : (b + 1) * PASS]
             else:
                 moving = even_w[b, a][:].bitcast(FP8X4)
@@ -249,35 +249,39 @@ def tile_list_orientation_energy_store_kernel(
                 MULT,
             )
 
-        respond("odd", 0, 0)
+        first = [(c, 0, jt, take_bank()) for c in range(2) for jt in range(TILES)]
+        for c, b, jt, bank in first:
+            response_pass("odd", c, b, jt, 0, bank)
+        for c, b, jt, bank in first:
+            response_pass("odd", c, b, jt, 1, bank)
+            square_bank("odd", c, b, jt, bank)
         respond("odd", 0, 1)
-        respond("odd", 1, 0)
         respond("odd", 1, 1)
         respond("odd", 2, 0)
-        respond("odd", 2, 1)
         respond("even", 0, 0)
         respond("even", 1, 0)
         amplitude(0, 0)
-        respond("even", 0, 1)
+        respond("odd", 2, 1)
         amplitude(1, 0)
-        amplitude(0, 1)
+        respond("even", 0, 1)
         respond("even", 1, 1)
-        respond("odd", 3, 0)
+        amplitude(0, 1)
+        respond("even", 2, 0)
         pool_and_place(0, 0)
         amplitude(1, 1)
-        respond("odd", 3, 1)
         pool_and_place(0, 1)
-        respond("even", 2, 0)
-        pool_and_place(0, 2)
         respond("even", 2, 1)
-        pool_and_place(1, 0)
+        pool_and_place(0, 2)
         amplitude(2, 0)
-        pool_and_place(1, 1)
-        respond("even", 3, 0)
+        pool_and_place(1, 0)
+        respond("odd", 3, 0)
         amplitude(2, 1)
+        pool_and_place(1, 1)
+        respond("odd", 3, 1)
         pool_and_place(1, 2)
-        respond("even", 3, 1)
+        respond("even", 3, 0)
         pool_and_place(2, 0)
+        respond("even", 3, 1)
         amplitude(3, 0)
         pool_and_place(2, 1)
         amplitude(3, 1)

@@ -29,7 +29,8 @@ TILES = CHUNK // P
 PAGES = N // P
 LIST_COLS = CHUNK // 16
 BANKS = 8
-VECTOR_SUMS = ((1, 1), (2, 0),)
+HELD_SUMS = 4
+VECTOR_SUMS = ((1, 0), (1, 1),)
 
 
 def tile_list_orientation_energy_store_kernel(
@@ -118,29 +119,32 @@ def tile_list_orientation_energy_store_kernel(
         pick_words(2, 1, keep)
 
         even_w, even_sc = {}, {}
+        staging = [
+            keep.tile([P, K_PASSES * piece], BF16, name="staging0", align_bytes=64),
+            reuse.tile([P, K_PASSES * piece], BF16, name="staging1", align_bytes=64, offset=0),
+        ]
         for b in range(H_PASSES):
             for a in range(K_PASSES):
-                raw = keep.tile([P, piece], F32, name=f"even_raw{b}_{a}")
-                rows = w_even[a * PASS : (a + 1) * PASS, b * PASS : (b + 1) * PASS]
-                nc.sync.dma_start(
-                    out=raw[:].rearrange("p (i r) -> p i r", i=PACK), in_=rows.rearrange("(p i) r -> p i r", i=PACK)
-                )
-                if (b, a) == (H_PASSES - 1, K_PASSES - 1):
-                    rounded = reuse.tile([P, piece], BF16, name="even_bf_last", align_bytes=64, offset=0)
-                else:
-                    rounded = keep.tile([P, piece], BF16, name=f"even_bf{b}_{a}", tag=f"rounded{b}_{a}", align_bytes=64)
-                nc.vector.tensor_copy(
-                    out=rounded[:].rearrange("p (g u i) -> p g i u", u=4, i=PACK),
-                    in_=raw[:].rearrange("p (i g u) -> p g i u", i=PACK, u=4),
-                )
                 codes = keep.tile([P, PASS], U32, name=f"even_w{b}_{a}", align_bytes=64)
                 scales = keep.tile([P, PASS], U8, name=f"even_sc{b}_{a}", align_bytes=64)
-                nc.vector.quantize_mx(out=codes[:].bitcast(FP8X4), scales=scales[:], in_=rounded[:])
+                width = PASS // 2 if (b, a) == (H_PASSES - 1, K_PASSES - 1) else PASS
+                for first in range(0, PASS, width):
+                    raw = keep.tile([P, PACK * width], F32, name=f"even_raw{b}_{a}_{first}")
+                    rows = w_even[a * PASS : (a + 1) * PASS, b * PASS + first : b * PASS + first + width]
+                    nc.sync.dma_start(
+                        out=raw[:].rearrange("p (i r) -> p i r", i=PACK), in_=rows.rearrange("(p i) r -> p i r", i=PACK)
+                    )
+                    rounded = staging[b][:, a * piece + PACK * first : a * piece + PACK * (first + width)]
+                    nc.vector.tensor_copy(
+                        out=rounded.rearrange("p (g u i) -> p g i u", u=4, i=PACK),
+                        in_=raw[:].rearrange("p (i g u) -> p g i u", i=PACK, u=4),
+                    )
+                    nc.vector.quantize_mx(
+                        out=codes[:, first : first + width].bitcast(FP8X4),
+                        scales=scales[:, first : first + width],
+                        in_=rounded,
+                    )
                 even_w[b, a], even_sc[b, a] = codes, scales
-
-        for a in range(K_PASSES):
-            pick_scales(CHUNKS - 1, a, reuse, offset=a * 5 * CHUNK)
-        pick_words(CHUNKS - 1, 1, reuse, offset=CHUNK)
 
         gain = keep.tile([P, S], F32, name="gain")
         nc.sync.dma_start(out=gain[:], in_=wgo)
@@ -163,6 +167,7 @@ def tile_list_orientation_energy_store_kernel(
             return used[-1]
 
         squares, amp_w, amp_sc = {}, {}, {}
+        held_sums = []
 
         def response_pass(kind, c, b, jt, a, bank):
             cols = slice(jt * P, (jt + 1) * P)
@@ -191,8 +196,14 @@ def tile_list_orientation_energy_store_kernel(
             )
             squares[kind, c, b, jt] = [square]
             if kind == "even" and (c, b) in VECTOR_SUMS:
-                both = keep.tile([P, PACK, P], F32, name=f"both{c}_{b}_{jt}")
-                nc.vector.tensor_tensor(both[:], squares["odd", c, b, jt][0][:], square[:], ADD)
+                odd_square = squares["odd", c, b, jt][0]
+                if len(held_sums) < HELD_SUMS:
+                    at = 6 * CHUNK + len(held_sums) * 4 * PASS
+                    both = reuse.tile([P, PACK, P], F32, name=f"both{c}_{b}_{jt}", align_bytes=64, offset=at)
+                    held_sums.append(both)
+                else:
+                    both = odd_square
+                nc.vector.tensor_tensor(both[:], odd_square[:], square[:], ADD)
                 squares["odd", c, b, jt], squares["even", c, b, jt] = [], [both]
 
         def respond(kind, c, b):
@@ -255,33 +266,39 @@ def tile_list_orientation_energy_store_kernel(
         for c, b, jt, bank in first:
             response_pass("odd", c, b, jt, 1, bank)
             square_bank("odd", c, b, jt, bank)
+        def pick_last_chunk():
+            for a in range(K_PASSES):
+                pick_scales(CHUNKS - 1, a, reuse, offset=a * 5 * CHUNK)
+            pick_words(CHUNKS - 1, 1, reuse, offset=CHUNK)
+
         respond("odd", 0, 1)
         respond("odd", 1, 1)
         respond("odd", 2, 0)
+        respond("odd", 2, 1)
         respond("even", 0, 0)
         respond("even", 1, 0)
         amplitude(0, 0)
-        respond("odd", 2, 1)
-        amplitude(1, 0)
         respond("even", 0, 1)
         respond("even", 1, 1)
         amplitude(0, 1)
+        amplitude(1, 0)
+        pick_last_chunk()
         respond("even", 2, 0)
         pool_and_place(0, 0)
-        amplitude(1, 1)
         pool_and_place(0, 1)
+        amplitude(1, 1)
         respond("even", 2, 1)
         pool_and_place(0, 2)
         amplitude(2, 0)
-        pool_and_place(1, 0)
         respond("odd", 3, 0)
+        pool_and_place(1, 0)
         amplitude(2, 1)
-        pool_and_place(1, 1)
         respond("odd", 3, 1)
-        pool_and_place(1, 2)
+        pool_and_place(1, 1)
         respond("even", 3, 0)
-        pool_and_place(2, 0)
+        pool_and_place(1, 2)
         respond("even", 3, 1)
+        pool_and_place(2, 0)
         amplitude(3, 0)
         pool_and_place(2, 1)
         amplitude(3, 1)

@@ -217,16 +217,16 @@ def tile_list_orientation_energy_store_kernel(
             amp = keep.tile([P, CHUNK * PACK], BF16, name=f"amp{c}_{b}", align_bytes=64)
             for jt in range(TILES):
                 energy = take_bank()
-                terms = squares["odd", c, b, jt] + squares["even", c, b, jt]
-                for t in range(PACK):
-                    for i, term in enumerate(terms):
+                terms = squares["even", c, b, jt] + squares["odd", c, b, jt]
+                for i, term in enumerate(terms):
+                    for t in range(PACK):
                         nc.tensor.matmul(
                             energy[:, t * P : (t + 1) * P],
                             lhsT=term[:, t, :],
                             rhs=ident[:],
                             is_transpose=True,
-                            start=(i == 0),
-                            stop=(i == len(terms) - 1),
+                            start=(i == 0 and t == 0),
+                            stop=(i == len(terms) - 1 and t == PACK - 1),
                         )
                 nc.scalar.activation(
                     out=amp[:, jt * PASS : (jt + 1) * PASS].rearrange("p (j t) -> p j t", t=PACK),

@@ -51,10 +51,10 @@ def tile_list_orientation_energy_store_kernel(
 
         tab_sc = keep.tile([P, K_PASSES * T], U8, name="tab_sc", align_bytes=64)
         nc.gpsimd.memset(tab_sc[:].bitcast(I32), 0)
-        for q in range(4):
+        for r in range(4):
             nc.sync.dma_start(
-                out=tab_sc[32 * q : 32 * q + 4, :].bitcast(I32).rearrange("r (a t) -> r a t", a=K_PASSES),
-                in_=tab_scales[:, 4 * q : 4 * q + 4, :].rearrange("a r t -> r a t").bitcast(I32),
+                out=tab_sc[r:P:32, :].bitcast(I32).rearrange("q (a t) -> q a t", a=K_PASSES),
+                in_=tab_scales[:, r:16:4, :].rearrange("a q t -> q a t").bitcast(I32),
             )
         odd_w = [keep.tile([P, K_PASSES, 2 * PASS], U8, name=f"odd_w{b}", align_bytes=64) for b in range(H_PASSES)]
 
@@ -67,10 +67,10 @@ def tile_list_orientation_energy_store_kernel(
         load_odd_words(0)
         odd_sc = keep.tile([P, K_PASSES, H], U8, name="odd_sc", align_bytes=64)
         nc.gpsimd.memset(odd_sc[:].bitcast(I32), 0)
-        for q in range(4):
+        for r in range(4):
             nc.sync.dma_start(
-                out=odd_sc[32 * q : 32 * q + 4, :, :].bitcast(I32),
-                in_=w_odd_scales[:, 4 * q : 4 * q + 4, :].rearrange("a r c -> r a c").bitcast(I32),
+                out=odd_sc[r:P:32, :, :].bitcast(I32),
+                in_=w_odd_scales[:, r:16:4, :].rearrange("a q c -> q a c").bitcast(I32),
             )
         nc.sync.dma_start(out=tab_w[:, T:], in_=tab_words[1].rearrange("p t i -> p (t i)").bitcast(I32))
         load_odd_words(1)
@@ -107,8 +107,11 @@ def tile_list_orientation_energy_store_kernel(
             patch_w[c, a] = picked
 
         for a in range(K_PASSES):
-            for c in range(2):
-                pick_scales(c, a, keep)
+            both = keep.tile([P, 2 * CHUNK], U8, name=f"early_sc{a}", align_bytes=64)
+            nc.vector.tensor_copy(
+                out=both[:], in_=tab_sc[:, a * T : (a + 1) * T].indirect(pick_list[:, : 2 * LIST_COLS])
+            )
+            patch_sc[0, a], patch_sc[1, a] = both[:, :CHUNK], both[:, CHUNK:]
             for c in range(2):
                 pick_words(c, a, keep)
         late_w = keep.tile([P, 2 * CHUNK], U32, name="late_w", align_bytes=64)
@@ -124,9 +127,10 @@ def tile_list_orientation_energy_store_kernel(
             reuse.tile([P, K_PASSES * piece], BF16, name="staging1", align_bytes=64, offset=0),
         ]
         for b in range(H_PASSES):
+            codes = keep.tile([P, K_PASSES * PASS], U32, name=f"even_w{b}", align_bytes=64)
+            scales = keep.tile([P, K_PASSES * PASS], U8, name=f"even_sc{b}", align_bytes=64)
+            done = 0
             for a in range(K_PASSES):
-                codes = keep.tile([P, PASS], U32, name=f"even_w{b}_{a}", align_bytes=64)
-                scales = keep.tile([P, PASS], U8, name=f"even_sc{b}_{a}", align_bytes=64)
                 width = PASS // 2 if (b, a) == (H_PASSES - 1, K_PASSES - 1) else PASS
                 for first in range(0, PASS, width):
                     raw = keep.tile([P, PACK * width], F32, name=f"even_raw{b}_{a}_{first}")
@@ -134,17 +138,22 @@ def tile_list_orientation_energy_store_kernel(
                     nc.sync.dma_start(
                         out=raw[:].rearrange("p (i r) -> p i r", i=PACK), in_=rows.rearrange("(p i) r -> p i r", i=PACK)
                     )
-                    rounded = staging[b][:, a * piece + PACK * first : a * piece + PACK * (first + width)]
+                    end = a * PASS + first + width
                     nc.vector.tensor_copy(
-                        out=rounded.rearrange("p (g u i) -> p g i u", u=4, i=PACK),
+                        out=staging[b][:, PACK * (end - width) : PACK * end].rearrange(
+                            "p (g u i) -> p g i u", u=4, i=PACK
+                        ),
                         in_=raw[:].rearrange("p (i g u) -> p g i u", i=PACK, u=4),
                     )
-                    nc.vector.quantize_mx(
-                        out=codes[:, first : first + width].bitcast(FP8X4),
-                        scales=scales[:, first : first + width],
-                        in_=rounded,
-                    )
-                even_w[b, a], even_sc[b, a] = codes, scales
+                    if (b, a) != (0, 0):
+                        nc.vector.quantize_mx(
+                            out=codes[:, done:end].bitcast(FP8X4),
+                            scales=scales[:, done:end],
+                            in_=staging[b][:, PACK * done : PACK * end],
+                        )
+                        done = end
+                even_w[b, a] = codes[:, a * PASS : (a + 1) * PASS]
+                even_sc[b, a] = scales[:, a * PASS : (a + 1) * PASS]
 
         gain = keep.tile([P, S], F32, name="gain")
         nc.sync.dma_start(out=gain[:], in_=wgo)
@@ -175,8 +184,8 @@ def tile_list_orientation_energy_store_kernel(
                 moving = odd_w[b][:, a, :].bitcast(FP4X4)
                 moving_sc = odd_sc[:, a, b * PASS : (b + 1) * PASS]
             else:
-                moving = even_w[b, a][:].bitcast(FP8X4)
-                moving_sc = even_sc[b, a][:]
+                moving = even_w[b, a].bitcast(FP8X4)
+                moving_sc = even_sc[b, a]
             nc.tensor.matmul_mx(
                 out=bank[:],
                 lhsT=patch_w[c, a][:, cols].bitcast(FP8X4),
@@ -252,7 +261,10 @@ def tile_list_orientation_energy_store_kernel(
                     stop=(b == H_PASSES - 1),
                 )
             y = keep.tile([P, CHUNK], F32, name=f"y{c}_{n}")
-            nc.scalar.copy(out=y[:], in_=pooled)
+            if (c, n) == (0, 0):
+                nc.vector.tensor_copy(out=y[:], in_=pooled)
+            else:
+                nc.scalar.copy(out=y[:], in_=pooled)
             nc.vector.tensor_tensor(
                 pages[n][:].indirect(place_list[:, c * LIST_COLS : (c + 1) * LIST_COLS]),
                 y[:],

@@ -28,6 +28,7 @@ CHUNKS = S // CHUNK
 TILES = CHUNK // P
 PAGES = N // P
 LIST_COLS = CHUNK // 16
+GROUP = P // 2
 BANKS = 8
 HELD_SUMS = 4
 VECTOR_SUMS = ((1, 0), (1, 1),)
@@ -141,9 +142,9 @@ def tile_list_orientation_energy_store_kernel(
                     end = a * PASS + first + width
                     nc.vector.tensor_copy(
                         out=staging[b][:, PACK * (end - width) : PACK * end].rearrange(
-                            "p (g u i) -> p g i u", u=4, i=PACK
+                            "p (h t m i) -> p h m i t", t=PACK, m=GROUP, i=PACK
                         ),
-                        in_=raw[:].rearrange("p (i g u) -> p g i u", i=PACK, u=4),
+                        in_=raw[:].rearrange("p (i h m t) -> p h m i t", i=PACK, m=GROUP, t=PACK),
                     )
                     if (b, a) != (0, 0):
                         nc.vector.quantize_mx(
@@ -198,11 +199,13 @@ def tile_list_orientation_energy_store_kernel(
 
         def square_bank(kind, c, b, jt, bank):
             square = keep.tile([P, PACK, P], F32, name=f"{kind}_sq{c}_{b}_{jt}")
-            nc.scalar.activation(
-                out=square[:].rearrange("p t (g u) -> p g t u", u=4),
-                in_=bank[:].rearrange("p (g u t) -> p g t u", u=4, t=PACK),
-                func=ACT.Square,
-            )
+            if kind == "odd":
+                sorted_out = square[:].rearrange("p t (g u) -> p g t u", u=4)
+                sorted_in = bank[:].rearrange("p (g u t) -> p g t u", u=4, t=PACK)
+            else:
+                sorted_out = square[:].rearrange("p t (h m) -> p h t m", m=GROUP)
+                sorted_in = bank[:].rearrange("p (h t m) -> p h t m", t=PACK, m=GROUP)
+            nc.scalar.activation(out=sorted_out, in_=sorted_in, func=ACT.Square)
             squares[kind, c, b, jt] = [square]
             if kind == "even" and (c, b) in VECTOR_SUMS:
                 odd_square = squares["odd", c, b, jt][0]
@@ -238,8 +241,8 @@ def tile_list_orientation_energy_store_kernel(
                             stop=(i == len(terms) - 1 and t == PACK - 1),
                         )
                 nc.scalar.activation(
-                    out=amp[:, jt * PASS : (jt + 1) * PASS].rearrange("p (j t) -> p j t", t=PACK),
-                    in_=energy[:].rearrange("p (t j) -> p j t", t=PACK),
+                    out=amp[:, jt * PASS : (jt + 1) * PASS].rearrange("p (g u t) -> p g t u", u=4, t=PACK),
+                    in_=energy[:].rearrange("p (t g u) -> p g t u", t=PACK, u=4),
                     func=ACT.Sqrt,
                 )
             codes = keep.tile([P, CHUNK], U32, name=f"amp_w{c}_{b}", align_bytes=64)

@@ -28,10 +28,14 @@ CHUNKS = S // CHUNK
 TILES = CHUNK // P
 PAGES = N // P
 LIST_COLS = CHUNK // 16
-GROUP = P // 2
+LAST_RAW_AT = 8192
+FIRST_AMP_AT = 12288
+LAST_W_AT = LAST_RAW_AT + 512
+FIRST_SQ_AT = 14336
 BANKS = 8
-HELD_SUMS = 4
-VECTOR_SUMS = ((1, 0), (1, 1),)
+VECTOR_COPIES = ((0, 0),)
+HELD_SUMS = 0
+VECTOR_SUMS = ()
 
 
 def tile_list_orientation_energy_store_kernel(
@@ -44,11 +48,11 @@ def tile_list_orientation_energy_store_kernel(
         psum = ctx.enter_context(tc.psum_pool(name="psum", bufs=1))
 
         pick_list = keep.tile([P, S // 16], U16, name="pick_list")
-        nc.sync.dma_start(pick_list[:], offs)
 
         piece = PACK * PASS
         tab_w = keep.tile([P, K_PASSES * T], I32, name="tab_w", align_bytes=64)
         nc.sync.dma_start(out=tab_w[:, :T], in_=tab_words[0].rearrange("p t i -> p (t i)").bitcast(I32))
+        nc.sync.dma_start(pick_list[:], offs)
 
         tab_sc = keep.tile([P, K_PASSES * T], U8, name="tab_sc", align_bytes=64)
         nc.gpsimd.memset(tab_sc[:].bitcast(I32), 0)
@@ -65,7 +69,7 @@ def tile_list_orientation_energy_store_kernel(
                 in_=w_odd_words[:, :, 2 * b * PASS : 2 * (b + 1) * PASS].rearrange("a p c -> p a c").bitcast(I32),
             )
 
-        load_odd_words(0)
+        load_odd_words(1)
         odd_sc = keep.tile([P, K_PASSES, H], U8, name="odd_sc", align_bytes=64)
         nc.gpsimd.memset(odd_sc[:].bitcast(I32), 0)
         for r in range(4):
@@ -74,53 +78,57 @@ def tile_list_orientation_energy_store_kernel(
                 in_=w_odd_scales[:, r:16:4, :].rearrange("a q c -> q a c").bitcast(I32),
             )
         nc.sync.dma_start(out=tab_w[:, T:], in_=tab_words[1].rearrange("p t i -> p (t i)").bitcast(I32))
-        load_odd_words(1)
+        load_odd_words(0)
 
         ident = keep.tile([P, P], F32, name="ident")
         make_identity(nc, ident[:])
-        pages = []
-        for n in range(PAGES):
-            page = keep.tile([P, T2], F32, name=f"page{n}")
+        sorted_w = keep.tile([P, K_PASSES * 2 * PASS], U8, name="sorted_w", align_bytes=64)
+        sorted_sc = keep.tile([P, K_PASSES * PASS], U8, name="sorted_sc", align_bytes=64)
+        for a in range(K_PASSES):
+            nc.gpsimd.tensor_copy(
+                out=sorted_sc[:, a * PASS : (a + 1) * PASS].rearrange("p (t m) -> p t m", t=PACK),
+                in_=odd_sc[:, a, :PASS].rearrange("p (m t) -> p t m", t=PACK),
+            )
+        for a in range(K_PASSES):
+            nc.gpsimd.tensor_copy(
+                out=sorted_w[:, a * 2 * PASS : (a + 1) * 2 * PASS].rearrange("p (t m x) -> p t m x", t=PACK, x=2),
+                in_=odd_w[0][:, a, :].rearrange("p (m t x) -> p t m x", t=PACK, x=2),
+            )
+        pages = [keep.tile([P, T2], F32, name=f"page{n}") for n in range(PAGES)]
+        for page in pages[:-1]:
             nc.gpsimd.memset(page[:], 0.0)
-            pages.append(page)
+        nc.vector.memset(pages[-1][:], 0.0)
 
         warm_in = keep.tile([P, 1], F32, name="warm_in")
         warm_out = keep.tile([P, 1], F32, name="warm_out")
         nc.vector.memset(warm_in[:], 1.0)
         nc.scalar.activation(out=warm_out[:], in_=warm_in[:], func=ACT.Sqrt)
 
+        early_w = [keep.tile([P, S - a * CHUNK], U32, name=f"early_w{a}", align_bytes=64) for a in range(K_PASSES)]
+        early_sc = [keep.tile([P, S - CHUNK], U8, name=f"early_sc{a}", align_bytes=64) for a in range(K_PASSES)]
         patch_w, patch_sc = {}, {}
 
-        def pick_scales(c, a, pool, offset=None):
-            picked = pool.tile([P, CHUNK], U8, name=f"patch_sc{c}_{a}", align_bytes=64, offset=offset)
-            nc.vector.tensor_copy(
-                out=picked[:],
-                in_=tab_sc[:, a * T : (a + 1) * T].indirect(pick_list[:, c * LIST_COLS : (c + 1) * LIST_COLS]),
-            )
-            patch_sc[c, a] = picked
+        def entries(first, count):
+            return pick_list[:, first * LIST_COLS : (first + count) * LIST_COLS]
 
-        def pick_words(c, a, pool, offset=None):
-            picked = pool.tile([P, CHUNK], U32, name=f"patch_w{c}_{a}", align_bytes=64, offset=offset)
-            nc.vector.tensor_copy(
-                out=picked[:],
-                in_=tab_w[:, a * T : (a + 1) * T].bitcast(U32).indirect(pick_list[:, c * LIST_COLS : (c + 1) * LIST_COLS]),
-            )
-            patch_w[c, a] = picked
+        def pick_scales(picked, a, first, count):
+            nc.vector.tensor_copy(out=picked, in_=tab_sc[:, a * T : (a + 1) * T].indirect(entries(first, count)))
+            for c in range(count):
+                patch_sc[first + c, a] = picked[:, c * CHUNK : (c + 1) * CHUNK]
+
+        def pick_words(picked, window, a, first, count):
+            nc.vector.tensor_copy(out=picked, in_=window.bitcast(U32).indirect(entries(first, count)))
+            for c in range(count):
+                patch_w[first + c, a] = picked[:, c * CHUNK : (c + 1) * CHUNK]
 
         for a in range(K_PASSES):
-            both = keep.tile([P, 2 * CHUNK], U8, name=f"early_sc{a}", align_bytes=64)
-            nc.vector.tensor_copy(
-                out=both[:], in_=tab_sc[:, a * T : (a + 1) * T].indirect(pick_list[:, : 2 * LIST_COLS])
-            )
-            patch_sc[0, a], patch_sc[1, a] = both[:, :CHUNK], both[:, CHUNK:]
+            pick_scales(early_sc[a][:, : 2 * CHUNK], a, 0, 2)
             for c in range(2):
-                pick_words(c, a, keep)
-        late_w = keep.tile([P, 2 * CHUNK], U32, name="late_w", align_bytes=64)
-        nc.vector.tensor_copy(out=late_w[:], in_=tab_w[:].bitcast(U32).indirect(pick_list[:, 2 * LIST_COLS :]))
-        patch_w[2, 0], patch_w[3, 0] = late_w[:, :CHUNK], late_w[:, CHUNK:]
+                pick_words(early_w[a][:, c * CHUNK : (c + 1) * CHUNK], tab_w[:, a * T : (a + 1) * T], a, c, 1)
+        pick_words(early_w[0][:, 2 * CHUNK :], tab_w[:], 0, 2, 2)
         for a in range(K_PASSES):
-            pick_scales(2, a, keep)
-        pick_words(2, 1, keep)
+            pick_scales(early_sc[a][:, 2 * CHUNK :], a, 2, 1)
+        pick_words(early_w[1][:, 2 * CHUNK :], tab_w[:, T:], 1, 2, 1)
 
         even_w, even_sc = {}, {}
         staging = [
@@ -130,29 +138,34 @@ def tile_list_orientation_energy_store_kernel(
         for b in range(H_PASSES):
             codes = keep.tile([P, K_PASSES * PASS], U32, name=f"even_w{b}", align_bytes=64)
             scales = keep.tile([P, K_PASSES * PASS], U8, name=f"even_sc{b}", align_bytes=64)
-            done = 0
             for a in range(K_PASSES):
-                width = PASS // 2 if (b, a) == (H_PASSES - 1, K_PASSES - 1) else PASS
-                for first in range(0, PASS, width):
-                    raw = keep.tile([P, PACK * width], F32, name=f"even_raw{b}_{a}_{first}")
-                    rows = w_even[a * PASS : (a + 1) * PASS, b * PASS + first : b * PASS + first + width]
+                halves = 2 if (b, a) == (H_PASSES - 1, K_PASSES - 1) else 1
+                width, rows_m = PASS // halves, P // halves
+                rounded = staging[b][:, a * piece : (a + 1) * piece]
+                for h in range(halves):
+                    if h == 1:
+                        raw = reuse.tile([P, PACK * width], F32, name="last_raw", align_bytes=64, offset=LAST_RAW_AT)
+                    else:
+                        raw = keep.tile([P, PACK * width], F32, name=f"even_raw{b}_{a}_{h}")
+                    rows = w_even[a * PASS : (a + 1) * PASS, b * PASS + h * width : b * PASS + (h + 1) * width]
                     nc.sync.dma_start(
                         out=raw[:].rearrange("p (i r) -> p i r", i=PACK), in_=rows.rearrange("(p i) r -> p i r", i=PACK)
                     )
-                    end = a * PASS + first + width
                     nc.vector.tensor_copy(
-                        out=staging[b][:, PACK * (end - width) : PACK * end].rearrange(
-                            "p (h t m i) -> p h m i t", t=PACK, m=GROUP, i=PACK
-                        ),
-                        in_=raw[:].rearrange("p (i h m t) -> p h m i t", i=PACK, m=GROUP, t=PACK),
+                        out=rounded.rearrange("p (t m i) -> p m i t", t=PACK, i=PACK)[:, h * rows_m : (h + 1) * rows_m],
+                        in_=raw[:].rearrange("p (i m t) -> p m i t", i=PACK, t=PACK),
                     )
-                    if (b, a) != (0, 0):
+                    if halves == 2:
+                        runs = [(a * PASS + t * P + h * rows_m, rows_m) for t in range(PACK)]
+                    else:
+                        runs = [(a * PASS, PASS)]
+                    for first, count in runs:
+                        cols = slice(first, first + count)
                         nc.vector.quantize_mx(
-                            out=codes[:, done:end].bitcast(FP8X4),
-                            scales=scales[:, done:end],
-                            in_=staging[b][:, PACK * done : PACK * end],
+                            out=codes[:, cols].bitcast(FP8X4),
+                            scales=scales[:, cols],
+                            in_=staging[b][:, PACK * first : PACK * (first + count)],
                         )
-                        done = end
                 even_w[b, a] = codes[:, a * PASS : (a + 1) * PASS]
                 even_sc[b, a] = scales[:, a * PASS : (a + 1) * PASS]
 
@@ -176,7 +189,9 @@ def tile_list_orientation_energy_store_kernel(
             used.append(banks[len(used) % BANKS])
             return used[-1]
 
-        squares, amp_w, amp_sc = {}, {}, {}
+        squares = {}
+        amp_w = [keep.tile([P, S], U32, name=f"amp_w{b}", align_bytes=64) for b in range(H_PASSES)]
+        amp_sc = [keep.tile([P, S], U8, name=f"amp_sc{b}", align_bytes=64) for b in range(H_PASSES)]
         held_sums = []
 
         def response_pass(kind, c, b, jt, a, bank):
@@ -198,19 +213,23 @@ def tile_list_orientation_energy_store_kernel(
             )
 
         def square_bank(kind, c, b, jt, bank):
-            square = keep.tile([P, PACK, P], F32, name=f"{kind}_sq{c}_{b}_{jt}")
+            if (kind, b, jt) == ("odd", 1, TILES - 1) and c < 2:
+                at = FIRST_SQ_AT + c * 4 * PASS
+                square = reuse.tile([P, PACK, P], F32, name=f"held_sq{c}", align_bytes=64, offset=at)
+            else:
+                square = keep.tile([P, PACK, P], F32, name=f"{kind}_sq{c}_{b}_{jt}")
             if kind == "odd":
                 sorted_out = square[:].rearrange("p t (g u) -> p g t u", u=4)
                 sorted_in = bank[:].rearrange("p (g u t) -> p g t u", u=4, t=PACK)
             else:
-                sorted_out = square[:].rearrange("p t (h m) -> p h t m", m=GROUP)
-                sorted_in = bank[:].rearrange("p (h t m) -> p h t m", t=PACK, m=GROUP)
+                sorted_out = square[:].rearrange("p t m -> p (t m)")
+                sorted_in = bank[:]
             nc.scalar.activation(out=sorted_out, in_=sorted_in, func=ACT.Square)
             squares[kind, c, b, jt] = [square]
             if kind == "even" and (c, b) in VECTOR_SUMS:
                 odd_square = squares["odd", c, b, jt][0]
                 if len(held_sums) < HELD_SUMS:
-                    at = 6 * CHUNK + len(held_sums) * 4 * PASS
+                    at = 0
                     both = reuse.tile([P, PACK, P], F32, name=f"both{c}_{b}_{jt}", align_bytes=64, offset=at)
                     held_sums.append(both)
                 else:
@@ -218,15 +237,18 @@ def tile_list_orientation_energy_store_kernel(
                 nc.vector.tensor_tensor(both[:], odd_square[:], square[:], ADD)
                 squares["odd", c, b, jt], squares["even", c, b, jt] = [], [both]
 
-        def respond(kind, c, b):
+        def respond(kind, c, b, again=None):
             for jt in range(TILES):
-                bank = take_bank()
+                bank = take_bank() if again is None else again[jt]
                 for a in range(K_PASSES):
                     response_pass(kind, c, b, jt, a, bank)
                 square_bank(kind, c, b, jt, bank)
 
         def amplitude(c, b):
-            amp = keep.tile([P, CHUNK * PACK], BF16, name=f"amp{c}_{b}", align_bytes=64)
+            if (c, b) == (0, 1):
+                amp = reuse.tile([P, CHUNK * PACK], BF16, name="first_amp", align_bytes=64, offset=FIRST_AMP_AT)
+            else:
+                amp = keep.tile([P, CHUNK * PACK], BF16, name=f"amp{c}_{b}", align_bytes=64)
             for jt in range(TILES):
                 energy = take_bank()
                 terms = squares["even", c, b, jt] + squares["odd", c, b, jt]
@@ -245,81 +267,124 @@ def tile_list_orientation_energy_store_kernel(
                     in_=energy[:].rearrange("p (t g u) -> p g t u", t=PACK, u=4),
                     func=ACT.Sqrt,
                 )
-            codes = keep.tile([P, CHUNK], U32, name=f"amp_w{c}_{b}", align_bytes=64)
-            scales = keep.tile([P, CHUNK], U8, name=f"amp_sc{c}_{b}", align_bytes=64)
-            nc.vector.quantize_mx(out=codes[:].bitcast(FP8X4), scales=scales[:], in_=amp[:])
-            amp_w[c, b], amp_sc[c, b] = codes, scales
+            quantise(c, b, amp)
 
-        def pool_and_place(c, n):
+        def quantise(c, b, amp):
+            cols = slice(c * CHUNK, (c + 1) * CHUNK)
+            nc.vector.quantize_mx(out=amp_w[b][:, cols].bitcast(FP8X4), scales=amp_sc[b][:, cols], in_=amp[:])
+
+        wide = {kind: keep.tile([P, PACK, 2 * CHUNK], F32, name=f"wide_{kind}") for kind in ("odd", "even")}
+
+        wide_sum = reuse.tile([P, PACK, 2 * CHUNK], F32, name="wide_sum", align_bytes=64, offset=0)
+
+        def respond_wide(kind, t):
+            bank = take_bank()
+            for a in range(K_PASSES):
+                if kind == "odd":
+                    fixed = sorted_w[:, 2 * (a * PASS + t * P) : 2 * (a * PASS + (t + 1) * P)].bitcast(FP4X4)
+                    fixed_sc = sorted_sc[:, a * PASS + t * P : a * PASS + (t + 1) * P]
+                else:
+                    fixed = even_w[0, a][:, t * P : (t + 1) * P].bitcast(FP8X4)
+                    fixed_sc = even_sc[0, a][:, t * P : (t + 1) * P]
+                nc.tensor.matmul_mx(
+                    out=bank[:],
+                    lhsT=fixed,
+                    lhsT_scale=fixed_sc,
+                    rhs=early_w[a][:, CHUNK : 3 * CHUNK].bitcast(FP8X4),
+                    rhs_scale=early_sc[a][:, CHUNK : 3 * CHUNK],
+                    start=(a == 0),
+                    stop=(a == K_PASSES - 1),
+                )
+            nc.scalar.activation(out=wide[kind][:, t, :], in_=bank[:], func=ACT.Square)
+            if kind == "even":
+                nc.vector.tensor_tensor(wide_sum[:, t, :], wide["odd"][:, t, :], wide["even"][:, t, :], ADD)
+
+        def amplitude_wide(c):
+            at = FIRST_SQ_AT + (c - 1) * 4 * PASS
+            amp = reuse.tile([P, CHUNK * PACK], BF16, name=f"wide_amp{c}", align_bytes=64, offset=at)
+            nc.scalar.activation(
+                out=amp[:].rearrange("p (g u t) -> p g t u", u=4, t=PACK),
+                in_=wide_sum[:, :, (c - 1) * CHUNK : c * CHUNK].rearrange("p t (g u) -> p g t u", u=4),
+                func=ACT.Sqrt,
+            )
+            quantise(c, 0, amp)
+
+        def pool_and_place(c, n, bank=None, count=1):
             cols = slice(n * P, (n + 1) * P)
-            pooled = take_bank()[:, :CHUNK]
+            pooled = (take_bank() if bank is None else bank)[:, : count * CHUNK]
+            span = slice(c * CHUNK, (c + count) * CHUNK)
             for b in range(H_PASSES):
                 nc.tensor.matmul_mx(
                     out=pooled,
                     lhsT=pool_w[:, b, cols].bitcast(FP8X4),
                     lhsT_scale=pool_sc[4 * b : P, cols],
-                    rhs=amp_w[c, b][:].bitcast(FP8X4),
-                    rhs_scale=amp_sc[c, b][:],
+                    rhs=amp_w[b][:, span].bitcast(FP8X4),
+                    rhs_scale=amp_sc[b][:, span],
                     start=(b == 0),
                     stop=(b == H_PASSES - 1),
                 )
-            y = keep.tile([P, CHUNK], F32, name=f"y{c}_{n}")
-            if (c, n) == (0, 0):
+            y = keep.tile([P, count * CHUNK], F32, name=f"y{c}_{n}")
+            if (c, n) in VECTOR_COPIES:
                 nc.vector.tensor_copy(out=y[:], in_=pooled)
             else:
                 nc.scalar.copy(out=y[:], in_=pooled)
             nc.vector.tensor_tensor(
-                pages[n][:].indirect(place_list[:, c * LIST_COLS : (c + 1) * LIST_COLS]),
+                pages[n][:].indirect(place_list[:, c * LIST_COLS : (c + count) * LIST_COLS]),
                 y[:],
-                gain[:, c * CHUNK : (c + 1) * CHUNK],
+                gain[:, span],
                 MULT,
             )
 
-        first = [(c, 0, jt, take_bank()) for c in range(2) for jt in range(TILES)]
+        def pick_last_chunk():
+            for a in range(K_PASSES):
+                picked = reuse.tile([P, CHUNK], U8, name=f"last_sc{a}", align_bytes=64, offset=LAST_RAW_AT + a * CHUNK)
+                pick_scales(picked[:], a, CHUNKS - 1, 1)
+            picked = reuse.tile([P, CHUNK], U32, name="last_w", align_bytes=64, offset=LAST_W_AT)
+            pick_words(picked[:], tab_w[:, T:], 1, CHUNKS - 1, 1)
+
+        first = [(c, 1, jt, take_bank()) for c in range(2) for jt in range(TILES)]
         for c, b, jt, bank in first:
             response_pass("odd", c, b, jt, 0, bank)
         for c, b, jt, bank in first:
             response_pass("odd", c, b, jt, 1, bank)
             square_bank("odd", c, b, jt, bank)
-        def pick_last_chunk():
-            for a in range(K_PASSES):
-                pick_scales(CHUNKS - 1, a, reuse, offset=a * 5 * CHUNK)
-            pick_words(CHUNKS - 1, 1, reuse, offset=CHUNK)
-
-        respond("odd", 0, 1)
-        respond("odd", 1, 1)
-        respond("odd", 2, 0)
+        respond("odd", 0, 0)
         respond("odd", 2, 1)
+        respond_wide("odd", 0)
+        respond_wide("odd", 1)
+        respond_wide("odd", 2)
+        respond_wide("odd", 3)
         respond("even", 0, 0)
-        respond("even", 1, 0)
+        respond_wide("even", 0)
+        respond_wide("even", 1)
         amplitude(0, 0)
+        respond_wide("even", 2)
         respond("even", 0, 1)
-        respond("even", 1, 1)
+        respond_wide("even", 3)
         amplitude(0, 1)
-        amplitude(1, 0)
         pick_last_chunk()
-        respond("even", 2, 0)
+        respond("even", 1, 1)
         pool_and_place(0, 0)
-        pool_and_place(0, 1)
-        amplitude(1, 1)
+        amplitude_wide(1)
         respond("even", 2, 1)
+        amplitude(1, 1)
+        pool_and_place(0, 1)
+        amplitude_wide(2)
         pool_and_place(0, 2)
-        amplitude(2, 0)
         respond("odd", 3, 0)
         pool_and_place(1, 0)
         amplitude(2, 1)
-        respond("odd", 3, 1)
-        pool_and_place(1, 1)
         respond("even", 3, 0)
+        pool_and_place(1, 1)
+        respond("odd", 3, 1)
         pool_and_place(1, 2)
         respond("even", 3, 1)
-        pool_and_place(2, 0)
         amplitude(3, 0)
-        pool_and_place(2, 1)
+        pool_and_place(2, 0)
         amplitude(3, 1)
-        pool_and_place(2, 2)
+        pool_and_place(2, 1, used[-2])
         pool_and_place(3, 0)
         pool_and_place(3, 1)
-        pool_and_place(3, 2)
+        pool_and_place(2, 2, count=2)
         for n in range(PAGES):
             nc.sync.dma_start(out=out[n * P : (n + 1) * P, :], in_=pages[n][:])

@@ -185,14 +185,19 @@ def tile_list_orientation_energy_store_kernel(
         banks = [psum.tile([P, PASS], F32, name=f"bank{i}") for i in range(BANKS)]
         used = []
 
-        def take_bank():
-            used.append(banks[len(used) % BANKS])
+        def take_bank(back=BANKS):
+            banks.append(banks.pop(BANKS - back))
+            used.append(banks[-1])
             return used[-1]
 
         squares = {}
         amp_w = [keep.tile([P, S], U32, name=f"amp_w{b}", align_bytes=64) for b in range(H_PASSES)]
-        amp_sc = [keep.tile([P, S], U8, name=f"amp_sc{b}", align_bytes=64) for b in range(H_PASSES)]
-        held_sums = []
+        amp_sc = [
+            reuse.tile([P, S], U8, name="amp_sc0", align_bytes=64, offset=LAST_RAW_AT + 2560),
+            keep.tile([P, S], U8, name="amp_sc1", align_bytes=64),
+        ]
+        waiting = []
+        pooled_in = {}
 
         def response_pass(kind, c, b, jt, a, bank):
             cols = slice(jt * P, (jt + 1) * P)
@@ -213,7 +218,7 @@ def tile_list_orientation_energy_store_kernel(
             )
 
         def square_bank(kind, c, b, jt, bank):
-            if (kind, b, jt) == ("odd", 1, TILES - 1) and c < 2:
+            if (b, jt) == (1, TILES - 1) and (kind, c) in (("even", 0), ("odd", 1), ("odd", 3)):
                 at = FIRST_SQ_AT + c * 4 * PASS
                 square = reuse.tile([P, PACK, P], F32, name=f"held_sq{c}", align_bytes=64, offset=at)
             else:
@@ -226,16 +231,6 @@ def tile_list_orientation_energy_store_kernel(
                 sorted_in = bank[:]
             nc.scalar.activation(out=sorted_out, in_=sorted_in, func=ACT.Square)
             squares[kind, c, b, jt] = [square]
-            if kind == "even" and (c, b) in VECTOR_SUMS:
-                odd_square = squares["odd", c, b, jt][0]
-                if len(held_sums) < HELD_SUMS:
-                    at = 0
-                    both = reuse.tile([P, PACK, P], F32, name=f"both{c}_{b}_{jt}", align_bytes=64, offset=at)
-                    held_sums.append(both)
-                else:
-                    both = odd_square
-                nc.vector.tensor_tensor(both[:], odd_square[:], square[:], ADD)
-                squares["odd", c, b, jt], squares["even", c, b, jt] = [], [both]
 
         def respond(kind, c, b, again=None):
             for jt in range(TILES):
@@ -244,30 +239,43 @@ def tile_list_orientation_energy_store_kernel(
                     response_pass(kind, c, b, jt, a, bank)
                 square_bank(kind, c, b, jt, bank)
 
-        def amplitude(c, b):
-            if (c, b) == (0, 1):
-                amp = reuse.tile([P, CHUNK * PACK], BF16, name="first_amp", align_bytes=64, offset=FIRST_AMP_AT)
-            else:
-                amp = keep.tile([P, CHUNK * PACK], BF16, name=f"amp{c}_{b}", align_bytes=64)
+        opened = {}
+
+        def transpose_into(energy, terms, start, stop):
+            for q, term in enumerate(terms):
+                for t in range(PACK):
+                    nc.tensor.matmul(
+                        energy[:, t * P : (t + 1) * P],
+                        lhsT=term[:, t, :],
+                        rhs=ident[:],
+                        is_transpose=True,
+                        start=(start and q == 0 and t == 0),
+                        stop=(stop and q == len(terms) - 1 and t == PACK - 1),
+                    )
+
+        def open_energy(c, b):
             for jt in range(TILES):
-                energy = take_bank()
-                terms = squares["even", c, b, jt] + squares["odd", c, b, jt]
-                for i, term in enumerate(terms):
-                    for t in range(PACK):
-                        nc.tensor.matmul(
-                            energy[:, t * P : (t + 1) * P],
-                            lhsT=term[:, t, :],
-                            rhs=ident[:],
-                            is_transpose=True,
-                            start=(i == 0 and t == 0),
-                            stop=(i == len(terms) - 1 and t == PACK - 1),
-                        )
+                opened[c, b, jt] = take_bank(back=6)
+                transpose_into(opened[c, b, jt], squares["odd", c, b, jt], True, False)
+
+        def amplitude(c, b):
+            amp = keep.tile([P, CHUNK * PACK], BF16, name=f"amp{c}_{b}", align_bytes=64)
+            for jt in range(TILES):
+                if (c, b, jt) in opened:
+                    energy = opened[c, b, jt]
+                    transpose_into(energy, squares["even", c, b, jt], False, True)
+                else:
+                    energy = take_bank()
+                    transpose_into(energy, squares["even", c, b, jt] + squares["odd", c, b, jt], True, True)
                 nc.scalar.activation(
                     out=amp[:, jt * PASS : (jt + 1) * PASS].rearrange("p (g u t) -> p g t u", u=4, t=PACK),
                     in_=energy[:].rearrange("p (t g u) -> p g t u", t=PACK, u=4),
                     func=ACT.Sqrt,
                 )
-            quantise(c, b, amp)
+            if (c, b) == (0, 0):
+                waiting.append(amp)
+            else:
+                quantise(c, b, amp)
 
         def quantise(c, b, amp):
             cols = slice(c * CHUNK, (c + 1) * CHUNK)
@@ -276,6 +284,9 @@ def tile_list_orientation_energy_store_kernel(
         wide = {kind: keep.tile([P, PACK, 2 * CHUNK], F32, name=f"wide_{kind}") for kind in ("odd", "even")}
 
         wide_sum = reuse.tile([P, PACK, 2 * CHUNK], F32, name="wide_sum", align_bytes=64, offset=0)
+
+        def add_wide(engine, t):
+            engine.tensor_tensor(wide_sum[:, t, :], wide["odd"][:, t, :], wide["even"][:, t, :], ADD)
 
         def respond_wide(kind, t):
             bank = take_bank()
@@ -296,8 +307,6 @@ def tile_list_orientation_energy_store_kernel(
                     stop=(a == K_PASSES - 1),
                 )
             nc.scalar.activation(out=wide[kind][:, t, :], in_=bank[:], func=ACT.Square)
-            if kind == "even":
-                nc.vector.tensor_tensor(wide_sum[:, t, :], wide["odd"][:, t, :], wide["even"][:, t, :], ADD)
 
         def amplitude_wide(c):
             at = FIRST_SQ_AT + (c - 1) * 4 * PASS
@@ -309,7 +318,7 @@ def tile_list_orientation_energy_store_kernel(
             )
             quantise(c, 0, amp)
 
-        def pool_and_place(c, n, bank=None, count=1):
+        def pool(c, n, bank=None, count=1):
             cols = slice(n * P, (n + 1) * P)
             pooled = (take_bank() if bank is None else bank)[:, : count * CHUNK]
             span = slice(c * CHUNK, (c + count) * CHUNK)
@@ -323,7 +332,15 @@ def tile_list_orientation_energy_store_kernel(
                     start=(b == 0),
                     stop=(b == H_PASSES - 1),
                 )
-            y = keep.tile([P, count * CHUNK], F32, name=f"y{c}_{n}")
+            pooled_in[c, n] = pooled
+
+        def place(c, n, count=1):
+            pooled = pooled_in[c, n]
+            span = slice(c * CHUNK, (c + count) * CHUNK)
+            if (c, n) == (2, 1):
+                y = reuse.tile([P, CHUNK], F32, name="held_y", align_bytes=64, offset=FIRST_SQ_AT + 12 * PASS)
+            else:
+                y = keep.tile([P, count * CHUNK], F32, name=f"y{c}_{n}")
             if (c, n) in VECTOR_COPIES:
                 nc.vector.tensor_copy(out=y[:], in_=pooled)
             else:
@@ -342,6 +359,10 @@ def tile_list_orientation_energy_store_kernel(
             picked = reuse.tile([P, CHUNK], U32, name="last_w", align_bytes=64, offset=LAST_W_AT)
             pick_words(picked[:], tab_w[:, T:], 1, CHUNKS - 1, 1)
 
+        def pool_and_place(c, n, bank=None, count=1):
+            pool(c, n, bank, count)
+            place(c, n, count)
+
         first = [(c, 1, jt, take_bank()) for c in range(2) for jt in range(TILES)]
         for c, b, jt, bank in first:
             response_pass("odd", c, b, jt, 0, bank)
@@ -356,33 +377,40 @@ def tile_list_orientation_energy_store_kernel(
         respond_wide("odd", 3)
         respond("even", 0, 0)
         respond_wide("even", 0)
+        add_wide(nc.gpsimd, 0)
         respond_wide("even", 1)
         amplitude(0, 0)
+        open_energy(0, 1)
         respond_wide("even", 2)
         respond("even", 0, 1)
         respond_wide("even", 3)
         amplitude(0, 1)
         pick_last_chunk()
+        quantise(0, 0, waiting[0])
+        add_wide(nc.vector, 1)
+        add_wide(nc.vector, 2)
+        add_wide(nc.vector, 3)
         respond("even", 1, 1)
         pool_and_place(0, 0)
         amplitude_wide(1)
-        respond("even", 2, 1)
         amplitude(1, 1)
         pool_and_place(0, 1)
-        amplitude_wide(2)
+        respond("even", 2, 1)
         pool_and_place(0, 2)
+        amplitude_wide(2)
         respond("odd", 3, 0)
         pool_and_place(1, 0)
         amplitude(2, 1)
-        respond("even", 3, 0)
         pool_and_place(1, 1)
-        respond("odd", 3, 1)
+        respond("even", 3, 0)
         pool_and_place(1, 2)
+        respond("odd", 3, 1)
         respond("even", 3, 1)
-        amplitude(3, 0)
         pool_and_place(2, 0)
+        amplitude(3, 0)
+        pool(2, 1)
         amplitude(3, 1)
-        pool_and_place(2, 1, used[-2])
+        place(2, 1)
         pool_and_place(3, 0)
         pool_and_place(3, 1)
         pool_and_place(2, 2, count=2)

@@ -231,13 +231,20 @@ def tile_list_orientation_energy_store_kernel(
                 sorted_in = bank[:]
             nc.scalar.activation(out=sorted_out, in_=sorted_in, func=ACT.Square)
             squares[kind, c, b, jt] = [square]
+            if kind == "even" and (c, b, jt) in VECTOR_SUMS:
+                both = squares["odd", c, b, jt][0]
+                nc.vector.tensor_tensor(both[:], both[:], square[:], ADD)
+                squares["even", c, b, jt] = []
 
-        def respond(kind, c, b, again=None):
+        def respond_tile(kind, c, b, jt):
+            bank = take_bank()
+            for a in range(K_PASSES):
+                response_pass(kind, c, b, jt, a, bank)
+            square_bank(kind, c, b, jt, bank)
+
+        def respond(kind, c, b):
             for jt in range(TILES):
-                bank = take_bank() if again is None else again[jt]
-                for a in range(K_PASSES):
-                    response_pass(kind, c, b, jt, a, bank)
-                square_bank(kind, c, b, jt, bank)
+                respond_tile(kind, c, b, jt)
 
         opened = {}
 
@@ -288,15 +295,16 @@ def tile_list_orientation_energy_store_kernel(
         def add_wide(engine, t):
             engine.tensor_tensor(wide_sum[:, t, :], wide["odd"][:, t, :], wide["even"][:, t, :], ADD)
 
+        def sorted_weights(kind, a, t):
+            if kind == "odd":
+                at = a * PASS + t * P
+                return sorted_w[:, 2 * at : 2 * (at + P)].bitcast(FP4X4), sorted_sc[:, at : at + P]
+            return even_w[0, a][:, t * P : (t + 1) * P].bitcast(FP8X4), even_sc[0, a][:, t * P : (t + 1) * P]
+
         def respond_wide(kind, t):
             bank = take_bank()
             for a in range(K_PASSES):
-                if kind == "odd":
-                    fixed = sorted_w[:, 2 * (a * PASS + t * P) : 2 * (a * PASS + (t + 1) * P)].bitcast(FP4X4)
-                    fixed_sc = sorted_sc[:, a * PASS + t * P : a * PASS + (t + 1) * P]
-                else:
-                    fixed = even_w[0, a][:, t * P : (t + 1) * P].bitcast(FP8X4)
-                    fixed_sc = even_sc[0, a][:, t * P : (t + 1) * P]
+                fixed, fixed_sc = sorted_weights(kind, a, t)
                 nc.tensor.matmul_mx(
                     out=bank[:],
                     lhsT=fixed,
@@ -318,6 +326,40 @@ def tile_list_orientation_energy_store_kernel(
             )
             quantise(c, 0, amp)
 
+        last = {kind: keep.tile([P, PACK, CHUNK], F32, name=f"last_{kind}") for kind in ("odd", "even")}
+
+        def respond_last(kind):
+            width = P if kind == "odd" else CHUNK
+            for pair in range(0, PACK, 2):
+                bank = take_bank()
+                for t in (pair, pair + 1):
+                    for at in range(0, CHUNK, width):
+                        for a in range(K_PASSES):
+                            fixed, fixed_sc = sorted_weights(kind, a, t)
+                            nc.tensor.matmul_mx(
+                                out=bank[:, (t - pair) * CHUNK + at : (t - pair) * CHUNK + at + width],
+                                lhsT=fixed,
+                                lhsT_scale=fixed_sc,
+                                rhs=patch_w[CHUNKS - 1, a][:, at : at + width].bitcast(FP8X4),
+                                rhs_scale=patch_sc[CHUNKS - 1, a][:, at : at + width],
+                                start=(a == 0),
+                                stop=(a == K_PASSES - 1),
+                            )
+                squared = last[kind][:, pair : pair + 2, :]
+                nc.scalar.activation(out=squared.rearrange("p t j -> p (t j)"), in_=bank[:], func=ACT.Square)
+                if kind == "even":
+                    both = last["odd"][:, pair : pair + 2, :]
+                    nc.vector.tensor_tensor(both, both, squared, ADD)
+
+        def amplitude_last():
+            amp = reuse.tile([P, CHUNK * PACK], BF16, name="last_amp", align_bytes=64, offset=FIRST_SQ_AT + 12 * PASS)
+            nc.scalar.activation(
+                out=amp[:].rearrange("p (g u t) -> p g t u", u=4, t=PACK),
+                in_=last["odd"][:].rearrange("p t (g u) -> p g t u", u=4),
+                func=ACT.Sqrt,
+            )
+            quantise(CHUNKS - 1, 0, amp)
+
         def pool(c, n, bank=None, count=1):
             cols = slice(n * P, (n + 1) * P)
             pooled = (take_bank() if bank is None else bank)[:, : count * CHUNK]
@@ -337,7 +379,7 @@ def tile_list_orientation_energy_store_kernel(
         def place(c, n, count=1):
             pooled = pooled_in[c, n]
             span = slice(c * CHUNK, (c + count) * CHUNK)
-            if (c, n) == (2, 1):
+            if (c, n) == (9, 9):
                 y = reuse.tile([P, CHUNK], F32, name="held_y", align_bytes=64, offset=FIRST_SQ_AT + 12 * PASS)
             else:
                 y = keep.tile([P, count * CHUNK], F32, name=f"y{c}_{n}")
@@ -398,19 +440,18 @@ def tile_list_orientation_energy_store_kernel(
         respond("even", 2, 1)
         pool_and_place(0, 2)
         amplitude_wide(2)
-        respond("odd", 3, 0)
+        respond_last("odd")
         pool_and_place(1, 0)
         amplitude(2, 1)
         pool_and_place(1, 1)
-        respond("even", 3, 0)
+        respond_last("even")
         pool_and_place(1, 2)
         respond("odd", 3, 1)
         respond("even", 3, 1)
         pool_and_place(2, 0)
-        amplitude(3, 0)
-        pool(2, 1)
         amplitude(3, 1)
-        place(2, 1)
+        amplitude_last()
+        pool_and_place(2, 1, used[-1])
         pool_and_place(3, 0)
         pool_and_place(3, 1)
         pool_and_place(2, 2, count=2)

@@ -218,7 +218,7 @@ def tile_list_orientation_energy_store_kernel(
             )
 
         def square_bank(kind, c, b, jt, bank):
-            if (b, jt) == (1, TILES - 1) and (kind, c) in (("even", 0), ("odd", 1), ("odd", 3)):
+            if jt == TILES - 1 and (kind, c, b) in (("even", 0, 1), ("odd", 1, 1), ("odd", 3, 0)):
                 at = FIRST_SQ_AT + c * 4 * PASS
                 square = reuse.tile([P, PACK, P], F32, name=f"held_sq{c}", align_bytes=64, offset=at)
             else:
@@ -326,53 +326,58 @@ def tile_list_orientation_energy_store_kernel(
             )
             quantise(c, 0, amp)
 
-        last = {kind: keep.tile([P, PACK, CHUNK], F32, name=f"last_{kind}") for kind in ("odd", "even")}
+        last = {kind: keep.tile([P, PACK, P], F32, name=f"last_{kind}") for kind in ("odd", "even")}
 
         def respond_last(kind):
-            width = P if kind == "odd" else CHUNK
-            for pair in range(0, PACK, 2):
-                bank = take_bank()
-                for t in (pair, pair + 1):
-                    for at in range(0, CHUNK, width):
-                        for a in range(K_PASSES):
-                            fixed, fixed_sc = sorted_weights(kind, a, t)
-                            nc.tensor.matmul_mx(
-                                out=bank[:, (t - pair) * CHUNK + at : (t - pair) * CHUNK + at + width],
-                                lhsT=fixed,
-                                lhsT_scale=fixed_sc,
-                                rhs=patch_w[CHUNKS - 1, a][:, at : at + width].bitcast(FP8X4),
-                                rhs_scale=patch_sc[CHUNKS - 1, a][:, at : at + width],
-                                start=(a == 0),
-                                stop=(a == K_PASSES - 1),
-                            )
-                squared = last[kind][:, pair : pair + 2, :]
-                nc.scalar.activation(out=squared.rearrange("p t j -> p (t j)"), in_=bank[:], func=ACT.Square)
-                if kind == "even":
-                    both = last["odd"][:, pair : pair + 2, :]
-                    nc.vector.tensor_tensor(both, both, squared, ADD)
+            bank = take_bank()
+            for t in range(PACK):
+                for a in range(K_PASSES):
+                    fixed, fixed_sc = sorted_weights(kind, a, t)
+                    nc.tensor.matmul_mx(
+                        out=bank[:, t * P : (t + 1) * P],
+                        lhsT=fixed,
+                        lhsT_scale=fixed_sc,
+                        rhs=patch_w[CHUNKS - 1, a][:, :P].bitcast(FP8X4),
+                        rhs_scale=patch_sc[CHUNKS - 1, a][:, :P],
+                        start=(a == 0),
+                        stop=(a == K_PASSES - 1),
+                    )
+            nc.scalar.activation(out=last[kind][:].rearrange("p t j -> p (t j)"), in_=bank[:], func=ACT.Square)
+            if kind == "even":
+                nc.vector.tensor_tensor(last["odd"][:], last["odd"][:], last["even"][:], ADD)
+            respond_tile(kind, CHUNKS - 1, 0, 1)
 
         def amplitude_last():
             amp = reuse.tile([P, CHUNK * PACK], BF16, name="last_amp", align_bytes=64, offset=FIRST_SQ_AT + 12 * PASS)
-            nc.scalar.activation(
-                out=amp[:].rearrange("p (g u t) -> p g t u", u=4, t=PACK),
-                in_=last["odd"][:].rearrange("p t (g u) -> p g t u", u=4),
-                func=ACT.Sqrt,
-            )
+            for jt, energy in enumerate((last["odd"][:].rearrange("p t j -> p (t j)"), opened["last"][:])):
+                nc.scalar.activation(
+                    out=amp[:, jt * PASS : (jt + 1) * PASS].rearrange("p (g u t) -> p g t u", u=4, t=PACK),
+                    in_=energy.rearrange("p (t g u) -> p g t u", t=PACK, u=4),
+                    func=ACT.Sqrt,
+                )
             quantise(CHUNKS - 1, 0, amp)
+
+        def transpose_last():
+            opened["last"] = take_bank()
+            terms = squares["even", CHUNKS - 1, 0, 1] + squares["odd", CHUNKS - 1, 0, 1]
+            transpose_into(opened["last"], terms, True, True)
 
         def pool(c, n, bank=None, count=1):
             cols = slice(n * P, (n + 1) * P)
             pooled = (take_bank() if bank is None else bank)[:, : count * CHUNK]
             span = slice(c * CHUNK, (c + count) * CHUNK)
-            for b in range(H_PASSES):
+            passes = list(range(H_PASSES))
+            if c + count == CHUNKS:
+                passes.reverse()
+            for b in passes:
                 nc.tensor.matmul_mx(
                     out=pooled,
                     lhsT=pool_w[:, b, cols].bitcast(FP8X4),
                     lhsT_scale=pool_sc[4 * b : P, cols],
                     rhs=amp_w[b][:, span].bitcast(FP8X4),
                     rhs_scale=amp_sc[b][:, span],
-                    start=(b == 0),
-                    stop=(b == H_PASSES - 1),
+                    start=(b == passes[0]),
+                    stop=(b == passes[-1]),
                 )
             pooled_in[c, n] = pooled
 
@@ -449,9 +454,10 @@ def tile_list_orientation_energy_store_kernel(
         respond("odd", 3, 1)
         respond("even", 3, 1)
         pool_and_place(2, 0)
-        amplitude(3, 1)
+        transpose_last()
         amplitude_last()
-        pool_and_place(2, 1, used[-1])
+        amplitude(3, 1)
+        pool_and_place(2, 1, used[-2])
         pool_and_place(3, 0)
         pool_and_place(3, 1)
         pool_and_place(2, 2, count=2)

from contextlib import ExitStack

import concourse.mybir as mybir
from concourse.masks import make_identity

K, H, N, T, S, T2 = 1024, 1024, 384, 2048, 1024, 2048
FLOPS = 2 * 2 * K * H * S + 2 * H * N * S

F32 = mybir.dt.float32
BF16 = mybir.dt.bfloat16
I32 = mybir.dt.int32
U32 = mybir.dt.uint32
U16 = mybir.dt.uint16
U8 = mybir.dt.uint8
FP8X4 = mybir.dt.float8_e4m3fn_x4
FP4X4 = mybir.dt.float4_e2m1fn_x4
ACT = mybir.ActivationFunctionType
MULT = mybir.AluOpType.mult
ADD = mybir.AluOpType.add

P = 128
PACK = 4
PASS = P * PACK
K_PASSES = K // PASS
H_PASSES = H // PASS
CHUNK = 256
CHUNKS = S // CHUNK
TILES = CHUNK // P
PAGES = N // P
LIST_COLS = CHUNK // 16
LAST_RAW_AT = 8192
FIRST_AMP_AT = 12288
LAST_W_AT = LAST_RAW_AT + 512
FIRST_SQ_AT = 14336
BANKS = 8
VECTOR_COPIES = ((0, 0),)
HELD_SUMS = 0
VECTOR_SUMS = ()


def tile_list_orientation_energy_store_kernel(
    tc, tab_words, tab_scales, offs, w_even, w_odd_words, w_odd_scales, w_pool_words, w_pool_scales, wgo, offs2, out
):
    nc = tc.nc
    with ExitStack() as ctx:
        keep = ctx.enter_context(tc.tile_pool(name="keep", bufs=1))
        reuse = ctx.enter_context(tc.tile_pool(name="reuse", bufs=1))
        psum = ctx.enter_context(tc.psum_pool(name="psum", bufs=1))

        pick_list = keep.tile([P, S // 16], U16, name="pick_list")

        piece = PACK * PASS
        tab_w = keep.tile([P, K_PASSES * T], I32, name="tab_w", align_bytes=64)
        nc.sync.dma_start(out=tab_w[:, :T], in_=tab_words[0].rearrange("p t i -> p (t i)").bitcast(I32))
        nc.sync.dma_start(pick_list[:], offs)

        tab_sc = keep.tile([P, K_PASSES * T], U8, name="tab_sc", align_bytes=64)
        nc.gpsimd.memset(tab_sc[:].bitcast(I32), 0)
        for r in range(4):
            nc.sync.dma_start(
                out=tab_sc[r:P:32, :].bitcast(I32).rearrange("q (a t) -> q a t", a=K_PASSES),
                in_=tab_scales[:, r:16:4, :].rearrange("a q t -> q a t").bitcast(I32),
            )
        odd_w = [keep.tile([P, K_PASSES, 2 * PASS], U8, name=f"odd_w{b}", align_bytes=64) for b in range(H_PASSES)]

        def load_odd_words(b):
            nc.sync.dma_start(
                out=odd_w[b][:].bitcast(I32),
                in_=w_odd_words[:, :, 2 * b * PASS : 2 * (b + 1) * PASS].rearrange("a p c -> p a c").bitcast(I32),
            )

        load_odd_words(1)
        odd_sc = keep.tile([P, K_PASSES, H], U8, name="odd_sc", align_bytes=64)
        nc.gpsimd.memset(odd_sc[:].bitcast(I32), 0)
        for r in range(4):
            nc.sync.dma_start(
                out=odd_sc[r:P:32, :, :].bitcast(I32),
                in_=w_odd_scales[:, r:16:4, :].rearrange("a q c -> q a c").bitcast(I32),
            )
        nc.sync.dma_start(out=tab_w[:, T:], in_=tab_words[1].rearrange("p t i -> p (t i)").bitcast(I32))
        load_odd_words(0)

        ident = keep.tile([P, P], F32, name="ident")
        make_identity(nc, ident[:])
        sorted_w = keep.tile([P, K_PASSES * 2 * PASS], U8, name="sorted_w", align_bytes=64)
        sorted_sc = keep.tile([P, K_PASSES * PASS], U8, name="sorted_sc", align_bytes=64)
        for a in range(K_PASSES):
            nc.gpsimd.tensor_copy(
                out=sorted_sc[:, a * PASS : (a + 1) * PASS].rearrange("p (t m) -> p t m", t=PACK),
                in_=odd_sc[:, a, :PASS].rearrange("p (m t) -> p t m", t=PACK),
            )
        for a in range(K_PASSES):
            nc.gpsimd.tensor_copy(
                out=sorted_w[:, a * 2 * PASS : (a + 1) * 2 * PASS].rearrange("p (t m x) -> p t m x", t=PACK, x=2),
                in_=odd_w[0][:, a, :].rearrange("p (m t x) -> p t m x", t=PACK, x=2),
            )
        pages = [keep.tile([P, T2], F32, name=f"page{n}") for n in range(PAGES)]
        for page in pages[:-1]:
            nc.gpsimd.memset(page[:], 0.0)
        nc.vector.memset(pages[-1][:], 0.0)

        warm_in = keep.tile([P, 1], F32, name="warm_in")
        warm_out = keep.tile([P, 1], F32, name="warm_out")
        nc.vector.memset(warm_in[:], 1.0)
        nc.scalar.activation(out=warm_out[:], in_=warm_in[:], func=ACT.Sqrt)

        early_w = [keep.tile([P, S - a * CHUNK], U32, name=f"early_w{a}", align_bytes=64) for a in range(K_PASSES)]
        early_sc = [keep.tile([P, S - CHUNK], U8, name=f"early_sc{a}", align_bytes=64) for a in range(K_PASSES)]
        patch_w, patch_sc = {}, {}

        def entries(first, count):
            return pick_list[:, first * LIST_COLS : (first + count) * LIST_COLS]

        def pick_scales(picked, a, first, count):
            nc.vector.tensor_copy(out=picked, in_=tab_sc[:, a * T : (a + 1) * T].indirect(entries(first, count)))
            for c in range(count):
                patch_sc[first + c, a] = picked[:, c * CHUNK : (c + 1) * CHUNK]

        def pick_words(picked, window, a, first, count):
            nc.vector.tensor_copy(out=picked, in_=window.bitcast(U32).indirect(entries(first, count)))
            for c in range(count):
                patch_w[first + c, a] = picked[:, c * CHUNK : (c + 1) * CHUNK]

        for a in range(K_PASSES):
            pick_scales(early_sc[a][:, : 2 * CHUNK], a, 0, 2)
            for c in range(2):
                pick_words(early_w[a][:, c * CHUNK : (c + 1) * CHUNK], tab_w[:, a * T : (a + 1) * T], a, c, 1)
        pick_words(early_w[0][:, 2 * CHUNK :], tab_w[:], 0, 2, 2)
        for a in range(K_PASSES):
            pick_scales(early_sc[a][:, 2 * CHUNK :], a, 2, 1)
        pick_words(early_w[1][:, 2 * CHUNK :], tab_w[:, T:], 1, 2, 1)

        even_w, even_sc = {}, {}
        staging = [
            keep.tile([P, K_PASSES * piece], BF16, name="staging0", align_bytes=64),
            reuse.tile([P, K_PASSES * piece], BF16, name="staging1", align_bytes=64, offset=0),
        ]
        for b in range(H_PASSES):
            codes = keep.tile([P, K_PASSES * PASS], U32, name=f"even_w{b}", align_bytes=64)
            scales = keep.tile([P, K_PASSES * PASS], U8, name=f"even_sc{b}", align_bytes=64)
            for a in range(K_PASSES):
                halves = 2 if (b, a) == (H_PASSES - 1, K_PASSES - 1) else 1
                width, rows_m = PASS // halves, P // halves
                rounded = staging[b][:, a * piece : (a + 1) * piece]
                for h in range(halves):
                    if h == 1:
                        raw = reuse.tile([P, PACK * width], F32, name="last_raw", align_bytes=64, offset=LAST_RAW_AT)
                    else:
                        raw = keep.tile([P, PACK * width], F32, name=f"even_raw{b}_{a}_{h}")
                    rows = w_even[a * PASS : (a + 1) * PASS, b * PASS + h * width : b * PASS + (h + 1) * width]
                    nc.sync.dma_start(
                        out=raw[:].rearrange("p (i r) -> p i r", i=PACK), in_=rows.rearrange("(p i) r -> p i r", i=PACK)
                    )
                    nc.vector.tensor_copy(
                        out=rounded.rearrange("p (t m i) -> p m i t", t=PACK, i=PACK)[:, h * rows_m : (h + 1) * rows_m],
                        in_=raw[:].rearrange("p (i m t) -> p m i t", i=PACK, t=PACK),
                    )
                    if halves == 2:
                        runs = [(a * PASS + t * P + h * rows_m, rows_m) for t in range(PACK)]
                    else:
                        runs = [(a * PASS, PASS)]
                    for first, count in runs:
                        cols = slice(first, first + count)
                        nc.vector.quantize_mx(
                            out=codes[:, cols].bitcast(FP8X4),
                            scales=scales[:, cols],
                            in_=staging[b][:, PACK * first : PACK * (first + count)],
                        )
                even_w[b, a] = codes[:, a * PASS : (a + 1) * PASS]
                even_sc[b, a] = scales[:, a * PASS : (a + 1) * PASS]

        gain = keep.tile([P, S], F32, name="gain")
        nc.sync.dma_start(out=gain[:], in_=wgo)
        place_list = keep.tile([P, S // 16], U16, name="place_list")
        nc.sync.dma_start(place_list[:], offs2)
        pool_w = keep.tile([P, H_PASSES, N], I32, name="pool_w", align_bytes=64)
        nc.sync.dma_start(out=pool_w[:], in_=w_pool_words.rearrange("b p c i -> p b (c i)").bitcast(I32))
        pool_sc = keep.tile([P, N], U8, name="pool_sc", align_bytes=64)
        nc.gpsimd.memset(pool_sc[:].bitcast(I32), 0)
        for q in range(4):
            nc.sync.dma_start(
                out=pool_sc[32 * q : 32 * q + 8, :].bitcast(I32), in_=w_pool_scales[:, 4 * q : 4 * q + 4, :].bitcast(I32)
            )

        banks = [psum.tile([P, PASS], F32, name=f"bank{i}") for i in range(BANKS)]
        used = []

        def take_bank(back=BANKS):
            banks.append(banks.pop(BANKS - back))
            used.append(banks[-1])
            return used[-1]

        squares = {}
        amp_w = [keep.tile([P, S], U32, name=f"amp_w{b}", align_bytes=64) for b in range(H_PASSES)]
        amp_sc = [
            reuse.tile([P, S], U8, name="amp_sc0", align_bytes=64, offset=LAST_RAW_AT + 2560),
            keep.tile([P, S], U8, name="amp_sc1", align_bytes=64),
        ]
        waiting = []
        pooled_in = {}

        def response_pass(kind, c, b, jt, a, bank):
            cols = slice(jt * P, (jt + 1) * P)
            if kind == "odd":
                moving = odd_w[b][:, a, :].bitcast(FP4X4)
                moving_sc = odd_sc[:, a, b * PASS : (b + 1) * PASS]
            else:
                moving = even_w[b, a].bitcast(FP8X4)
                moving_sc = even_sc[b, a]
            nc.tensor.matmul_mx(
                out=bank[:],
                lhsT=patch_w[c, a][:, cols].bitcast(FP8X4),
                lhsT_scale=patch_sc[c, a][:, cols],
                rhs=moving,
                rhs_scale=moving_sc,
                start=(a == 0),
                stop=(a == K_PASSES - 1),
            )

        def square_bank(kind, c, b, jt, bank):
            if jt == TILES - 1 and (kind, c, b) in (("even", 0, 1), ("odd", 1, 1), ("odd", 3, 0)):
                at = FIRST_SQ_AT + c * 4 * PASS
                square = reuse.tile([P, PACK, P], F32, name=f"held_sq{c}", align_bytes=64, offset=at)
            else:
                square = keep.tile([P, PACK, P], F32, name=f"{kind}_sq{c}_{b}_{jt}")
            if kind == "odd":
                sorted_out = square[:].rearrange("p t (g u) -> p g t u", u=4)
                sorted_in = bank[:].rearrange("p (g u t) -> p g t u", u=4, t=PACK)
            else:
                sorted_out = square[:].rearrange("p t m -> p (t m)")
                sorted_in = bank[:]
            nc.scalar.activation(out=sorted_out, in_=sorted_in, func=ACT.Square)
            squares[kind, c, b, jt] = [square]
            if kind == "even" and (c, b, jt) in VECTOR_SUMS:
                both = squares["odd", c, b, jt][0]
                nc.vector.tensor_tensor(both[:], both[:], square[:], ADD)
                squares["even", c, b, jt] = []

        def respond_tile(kind, c, b, jt):
            bank = take_bank()
            for a in range(K_PASSES):
                response_pass(kind, c, b, jt, a, bank)
            square_bank(kind, c, b, jt, bank)

        def respond(kind, c, b):
            for jt in range(TILES):
                respond_tile(kind, c, b, jt)

        opened = {}

        def transpose_into(energy, terms, start, stop):
            for q, term in enumerate(terms):
                for t in range(PACK):
                    nc.tensor.matmul(
                        energy[:, t * P : (t + 1) * P],
                        lhsT=term[:, t, :],
                        rhs=ident[:],
                        is_transpose=True,
                        start=(start and q == 0 and t == 0),
                        stop=(stop and q == len(terms) - 1 and t == PACK - 1),
                    )

        def open_energy(c, b):
            for jt in range(TILES):
                opened[c, b, jt] = take_bank(back=6)
                transpose_into(opened[c, b, jt], squares["odd", c, b, jt], True, False)

        def amplitude(c, b):
            amp = keep.tile([P, CHUNK * PACK], BF16, name=f"amp{c}_{b}", align_bytes=64)
            for jt in range(TILES):
                if (c, b, jt) in opened:
                    energy = opened[c, b, jt]
                    transpose_into(energy, squares["even", c, b, jt], False, True)
                else:
                    energy = take_bank()
                    transpose_into(energy, squares["even", c, b, jt] + squares["odd", c, b, jt], True, True)
                nc.scalar.activation(
                    out=amp[:, jt * PASS : (jt + 1) * PASS].rearrange("p (g u t) -> p g t u", u=4, t=PACK),
                    in_=energy[:].rearrange("p (t g u) -> p g t u", t=PACK, u=4),
                    func=ACT.Sqrt,
                )
            if (c, b) == (0, 0):
                waiting.append(amp)
            else:
                quantise(c, b, amp)

        def quantise(c, b, amp):
            cols = slice(c * CHUNK, (c + 1) * CHUNK)
            nc.vector.quantize_mx(out=amp_w[b][:, cols].bitcast(FP8X4), scales=amp_sc[b][:, cols], in_=amp[:])

        wide = {kind: keep.tile([P, PACK, 2 * CHUNK], F32, name=f"wide_{kind}") for kind in ("odd", "even")}

        wide_sum = reuse.tile([P, PACK, 2 * CHUNK], F32, name="wide_sum", align_bytes=64, offset=0)

        def add_wide(engine, t):
            engine.tensor_tensor(wide_sum[:, t, :], wide["odd"][:, t, :], wide["even"][:, t, :], ADD)

        def sorted_weights(kind, a, t):
            if kind == "odd":
                at = a * PASS + t * P
                return sorted_w[:, 2 * at : 2 * (at + P)].bitcast(FP4X4), sorted_sc[:, at : at + P]
            return even_w[0, a][:, t * P : (t + 1) * P].bitcast(FP8X4), even_sc[0, a][:, t * P : (t + 1) * P]

        def respond_wide(kind, t):
            bank = take_bank()
            for a in range(K_PASSES):
                fixed, fixed_sc = sorted_weights(kind, a, t)
                nc.tensor.matmul_mx(
                    out=bank[:],
                    lhsT=fixed,
                    lhsT_scale=fixed_sc,
                    rhs=early_w[a][:, CHUNK : 3 * CHUNK].bitcast(FP8X4),
                    rhs_scale=early_sc[a][:, CHUNK : 3 * CHUNK],
                    start=(a == 0),
                    stop=(a == K_PASSES - 1),
                )
            nc.scalar.activation(out=wide[kind][:, t, :], in_=bank[:], func=ACT.Square)

        def amplitude_wide(c):
            at = FIRST_SQ_AT + (c - 1) * 4 * PASS
            amp = reuse.tile([P, CHUNK * PACK], BF16, name=f"wide_amp{c}", align_bytes=64, offset=at)
            nc.scalar.activation(
                out=amp[:].rearrange("p (g u t) -> p g t u", u=4, t=PACK),
                in_=wide_sum[:, :, (c - 1) * CHUNK : c * CHUNK].rearrange("p t (g u) -> p g t u", u=4),
                func=ACT.Sqrt,
            )
            quantise(c, 0, amp)

        last = {kind: keep.tile([P, PACK, P], F32, name=f"last_{kind}") for kind in ("odd", "even")}

        def respond_last(kind):
            bank = take_bank()
            for t in range(PACK):
                for a in range(K_PASSES):
                    fixed, fixed_sc = sorted_weights(kind, a, t)
                    nc.tensor.matmul_mx(
                        out=bank[:, t * P : (t + 1) * P],
                        lhsT=fixed,
                        lhsT_scale=fixed_sc,
                        rhs=patch_w[CHUNKS - 1, a][:, :P].bitcast(FP8X4),
                        rhs_scale=patch_sc[CHUNKS - 1, a][:, :P],
                        start=(a == 0),
                        stop=(a == K_PASSES - 1),
                    )
            nc.scalar.activation(out=last[kind][:].rearrange("p t j -> p (t j)"), in_=bank[:], func=ACT.Square)
            if kind == "even":
                nc.vector.tensor_tensor(last["odd"][:], last["odd"][:], last["even"][:], ADD)
            respond_tile(kind, CHUNKS - 1, 0, 1)

        def amplitude_last():
            amp = reuse.tile([P, CHUNK * PACK], BF16, name="last_amp", align_bytes=64, offset=FIRST_SQ_AT + 12 * PASS)
            for jt, energy in enumerate((last["odd"][:].rearrange("p t j -> p (t j)"), opened["last"][:])):
                nc.scalar.activation(
                    out=amp[:, jt * PASS : (jt + 1) * PASS].rearrange("p (g u t) -> p g t u", u=4, t=PACK),
                    in_=energy.rearrange("p (t g u) -> p g t u", t=PACK, u=4),
                    func=ACT.Sqrt,
                )
            quantise(CHUNKS - 1, 0, amp)

        def transpose_last():
            opened["last"] = take_bank()
            terms = squares["even", CHUNKS - 1, 0, 1] + squares["odd", CHUNKS - 1, 0, 1]
            transpose_into(opened["last"], terms, True, True)

        def pool(c, n, bank=None, count=1):
            cols = slice(n * P, (n + 1) * P)
            pooled = (take_bank() if bank is None else bank)[:, : count * CHUNK]
            span = slice(c * CHUNK, (c + count) * CHUNK)
            passes = list(range(H_PASSES))
            if c + count == CHUNKS:
                passes.reverse()
            for b in passes:
                nc.tensor.matmul_mx(
                    out=pooled,
                    lhsT=pool_w[:, b, cols].bitcast(FP8X4),
                    lhsT_scale=pool_sc[4 * b : P, cols],
                    rhs=amp_w[b][:, span].bitcast(FP8X4),
                    rhs_scale=amp_sc[b][:, span],
                    start=(b == passes[0]),
                    stop=(b == passes[-1]),
                )
            pooled_in[c, n] = pooled

        def place(c, n, count=1):
            pooled = pooled_in[c, n]
            span = slice(c * CHUNK, (c + count) * CHUNK)
            if (c, n) == (9, 9):
                y = reuse.tile([P, CHUNK], F32, name="held_y", align_bytes=64, offset=FIRST_SQ_AT + 12 * PASS)
            else:
                y = keep.tile([P, count * CHUNK], F32, name=f"y{c}_{n}")
            if (c, n) in VECTOR_COPIES:
                nc.vector.tensor_copy(out=y[:], in_=pooled)
            else:
                nc.scalar.copy(out=y[:], in_=pooled)
            nc.vector.tensor_tensor(
                pages[n][:].indirect(place_list[:, c * LIST_COLS : (c + count) * LIST_COLS]),
                y[:],
                gain[:, span],
                MULT,
            )

        def pick_last_chunk():
            for a in range(K_PASSES):
                picked = reuse.tile([P, CHUNK], U8, name=f"last_sc{a}", align_bytes=64, offset=LAST_RAW_AT + a * CHUNK)
                pick_scales(picked[:], a, CHUNKS - 1, 1)
            picked = reuse.tile([P, CHUNK], U32, name="last_w", align_bytes=64, offset=LAST_W_AT)
            pick_words(picked[:], tab_w[:, T:], 1, CHUNKS - 1, 1)

        def pool_and_place(c, n, bank=None, count=1):
            pool(c, n, bank, count)
            place(c, n, count)

        first = [(c, 1, jt, take_bank()) for c in range(2) for jt in range(TILES)]
        for c, b, jt, bank in first:
            response_pass("odd", c, b, jt, 0, bank)
        for c, b, jt, bank in first:
            response_pass("odd", c, b, jt, 1, bank)
            square_bank("odd", c, b, jt, bank)
        respond("odd", 0, 0)
        respond("odd", 2, 1)
        respond_wide("odd", 0)
        respond_wide("odd", 1)
        respond_wide("odd", 2)
        respond_wide("odd", 3)
        respond("even", 0, 0)
        respond_wide("even", 0)
        add_wide(nc.gpsimd, 0)
        respond_wide("even", 1)
        amplitude(0, 0)
        open_energy(0, 1)
        respond_wide("even", 2)
        respond("even", 0, 1)
        respond_wide("even", 3)
        amplitude(0, 1)
        pick_last_chunk()
        quantise(0, 0, waiting[0])
        add_wide(nc.vector, 1)
        add_wide(nc.vector, 2)
        add_wide(nc.vector, 3)
        respond("even", 1, 1)
        pool_and_place(0, 0)
        amplitude_wide(1)
        amplitude(1, 1)
        pool_and_place(0, 1)
        respond("even", 2, 1)
        pool_and_place(0, 2)
        amplitude_wide(2)
        respond_last("odd")
        pool_and_place(1, 0)
        amplitude(2, 1)
        pool_and_place(1, 1)
        respond_last("even")
        pool_and_place(1, 2)
        respond("odd", 3, 1)
        respond("even", 3, 1)
        pool_and_place(2, 0)
        transpose_last()
        amplitude_last()
        amplitude(3, 1)
        pool_and_place(2, 1, used[-2])
        pool_and_place(3, 0)
        pool_and_place(3, 1)
        pool_and_place(2, 2, count=2)
        for n in range(PAGES):
            nc.sync.dma_start(out=out[n * P : (n + 1) * P, :], in_=pages[n][:])
